import numpy as np, ml_dtypes
CORES = [36,164,52,180,100,228,116,244]
N = 8
import mx_ref
BF = ml_dtypes.bfloat16
def gentries(a):
    return np.ascontiguousarray(a.reshape(8, 16, -1).transpose(0, 2, 1)).reshape(8, -1)
def gtable(e):
    e = np.asarray(e); return np.ascontiguousarray(e.reshape(8, -1, 16).transpose(0, 2, 1)).reshape(128, -1).astype(np.int32)
def gcols(t, e):
    v = np.concatenate([t.reshape(8, 16, -1, 4), np.zeros((8, 16, 1, 4), BF)], axis=2)
    return np.ascontiguousarray(np.stack([v[g][:, e[g]] for g in range(8)])).reshape(128, -1)
def gpick(z, e):
    return np.concatenate([z[16 * g:16 * g + 16][:, e[g]] for g in range(8)])
def tile(rs):
    return np.stack(rs, axis=2).reshape(128, -1).astype(BF)
def pick(q, e):
    c = np.concatenate([q[0].reshape(128, -1, 4), np.zeros((128, 1, 4), np.uint8)], axis=1); s = np.concatenate([q[1], np.ones((16, 1), np.uint8)], axis=1)
    return (np.ascontiguousarray(c[:, e].reshape(128, -1)), np.ascontiguousarray(s[:, e]))
def join(*qs):
    return (np.concatenate([q[0] for q in qs], axis=1), np.concatenate([q[1] for q in qs], axis=1))
def put(q, e, v):
    c, s = q[0].reshape(128, -1, 4).copy(), q[1].copy(); c[:, e] = v[0].reshape(128, -1, 4); s[:, e] = v[1]
    return (c.reshape(128, -1), s)
def pk(c, s):
    return (np.ascontiguousarray(c), mx_ref.live(s))
def emit(q):
    return q[0], q[1]
def packed(v, rng):
    q = [mx_ref.quantize(np.ascontiguousarray(v[r])) for r in range(N)]
    return np.stack([a for a, b in q]), np.stack([mx_ref.plane(b, rng) for a, b in q])
def values_of_codes():
    e, c = np.zeros((128, 128, 4), np.float32), np.zeros((128, 2, 4), np.uint8)
    e[np.arange(128), np.arange(128), 0] = 1
    c[:127, :, 0] = np.arange(256).reshape(2, 128).T[:127]
    return mx_ref.matmul(mx_ref.quantize(e.reshape(128, 512).astype(BF)), (c.reshape(128, 8), np.full((16, 2), 127, np.uint8))).T.reshape(-1).astype(np.float64)
CODE_VALUE, SCALE_VALUE = values_of_codes(), 2.0 ** (np.arange(256) - 127.0)
def decode(q):
    return (CODE_VALUE[q[0]].reshape(16, 8, -1, 4) * SCALE_VALUE[q[1]][:, None, :, None] + 0.0).reshape(128, -1).astype(np.float32)
def f(rng, *shape):
    return mx_ref.flush((rng.standard_normal(shape, dtype=np.float32) * np.exp2(rng.integers(-2, 3, shape[:-1] + (1,)))).astype(BF))
def wide(rng, *shape, cols=0):
    v = rng.standard_normal(shape, dtype=np.float32) * np.exp2(rng.integers(-12, 13, shape)).astype(np.float32)
    if cols: v *= np.repeat(np.exp2(rng.integers(-cols, cols + 1, shape[:-2] + (1, shape[-1] // 4))) * (rng.random(shape[:-2] + (1, shape[-1] // 4)) > 0.0625), 4, axis=-1).astype(np.float32)
    return mx_ref.flush(v.astype(BF))
C, B = 256, 128
STEP = [1, 2, 4]
def big(v):
    v = v.astype(np.float32)
    v[np.abs(v) < np.float32(2.0 ** -16)] = 0
    return v.astype(BF)
def numbers_of(rng):
    return {"x": big(f(rng, N, 128, 4 * C)), "u": np.array(f(rng, N, 128, 512)), "v": np.array(f(rng, N, 128, 512))}
def layers(rng):
    k = np.stack([np.exp2(rng.permutation(128) % 5 - 2.0) for r in range(N)])[:, :, None].astype(np.float32)
    return big(rng.standard_normal((N, 128, 2048), dtype=np.float32) * k).reshape(N, 8, 16, 4, 8, 16, 4)
def weights(rng, w):
    c, p = packed(np.ascontiguousarray(w).reshape(N, 128, 2048), rng)
    return {"wc": c, "ws": p}
def still(w, parts):
    for i in parts:
        w[:, :, i] = 0
        w[:, :, :, :, :, i] = 0
    return w
def lists(rng, how, label):
    o, m = np.zeros((N, 8, C), int), np.zeros((N, 8, C), int)
    i = np.arange(B)
    for r in range(N):
        for g in range(8):
            e = rng.permutation(C)
            s, t = [(e[:B], e[B:]), (i, C - 1 - i), (i, B + i), (2 * i, 2 * i + 1), (2 * i + 1, (2 * i + 2) % C), (B + i, B - 1 - i)][how[r, g]]
            j, k = [(rng.permutation(B), rng.permutation(B)), (i, i), (B - 1 - i, B - 1 - i)][label[r, g]]
            o[r, g, s] = j
            o[r, g, t] = B + k
            m[r, g, j] = B + k
            m[r, g, B + k] = j
    return {"o": np.stack([gtable(o[r]) for r in range(N)]), "m": np.stack([gtable(m[r]) for r in range(N)])}
NONE = np.zeros((N, 8), int)
def setup_inputs(rng):
    return {**numbers_of(rng), **lists(rng, NONE, NONE), **weights(rng, layers(rng))}
def setup_inputs_ties(rng):
    d = numbers_of(rng)
    x = d["x"].reshape(N, 8, 16, C, 4)
    x[:, :, 0] = 0
    x[:, :, 0, :, 0] = rng.integers(0, 3, (N, 8, C)).astype(np.float32).astype(BF)
    u = d["u"].reshape(N, 128, 128, 4)
    u[:, :, ::16] = 0
    z = rng.permutation(N)
    for r in range(N):
        for h in range(0, 128, 16): u[r, h, h, 0] = 0.0 if z[r] == 0 else -1.0 if z[r] == 1 else 1.0
    how = (rng.permutation(N)[:, None] + np.arange(8)) % 6
    return {"x": x.reshape(N, 128, 4 * C), "u": u.reshape(N, 128, 512), "v": d["v"], **lists(rng, how, NONE), **weights(rng, still(layers(rng), [0]))}
def setup_inputs_near(rng):
    d = numbers_of(rng)
    x = d["x"].astype(np.float32).reshape(N, 8, 16, C, 4)
    x[:, :, 0] = 0
    x[:, :, 8:] = 0
    u = d["u"].reshape(N, 128, 128, 4)
    u[:, :, ::16] = 0
    z = rng.permutation(N) % 4
    for r in range(N):
        s = rng.integers(0, 16, (8, C))
        c = rng.integers(0, 2, (8, C)) * 2.0 - 1.0
        k = 1.0 if z[r] == 0 else 2.0 ** -30
        if z[r] < 3:
            x[r, :, 0, :, 0] = c if z[r] < 2 else c * (rng.random((8, C)) < 0.25)
            x[r, :, 8] = ((s[:, :, None] >> np.arange(4)) & 1) * np.exp2(np.arange(4) - 23.0)
        else:
            x[r, :, 10, :, 0] = (s % 2) * 1.125 * 2.0 ** -29
            x[r, :, 12, :, 0] = (1 - s % 2) * 2.0 ** -29
        if z[r] < 2: x[r, :, 11, :, 0] = 2.0 ** -10
        for h in range(0, 128, 16):
            if z[r] < 3:
                u[r, h, h, 0] = 1.0 if z[r] == 2 else k
                u[r, h + 8, h] = k
                u[r, h + 11, h, 0] = k
            else:
                u[r, h + 10, h, 0] = 1.125 * k
                u[r, h + 12, h, 0] = 1.25 * k
    return {"x": x.reshape(N, 128, 4 * C).astype(BF), "u": u.reshape(N, 128, 512), "v": d["v"], **lists(rng, NONE, NONE), **weights(rng, still(layers(rng), [0, 8, 9, 10, 11, 12, 13, 14, 15]))}
def setup_inputs_fine(rng):
    d = numbers_of(rng)
    e = rng.integers(8, 15, (N, 8, 16, C, 4))
    e[:, :, 1] = (8 + (np.arange(N)[:, None] + np.arange(8)) % 7)[:, :, None, None]
    x = (1.125 + 0.25 * rng.integers(0, 4, (N, 8, 16, C, 4))) * np.exp2(-e.astype(np.float64))
    x[:, :, ::8, :, 0] = 1.96875
    x *= rng.integers(0, 2, x.shape) * 2.0 - 1.0
    x *= np.exp2(rng.integers(-2, 3, (N, 1, 1, C, 1)).astype(np.float64))
    u = d["u"].reshape(N, 128, 128, 4)
    u[:, :, ::16] = 0
    for h in range(0, 128, 16): u[:, h + 1, h] = 1.0
    w = layers(rng)
    w[:, :, ::8, :, :, :, 0] = 0
    return {"x": x.astype(np.float32).reshape(N, 128, 4 * C).astype(BF), "u": u.reshape(N, 128, 512), "v": d["v"], **lists(rng, NONE, NONE), **weights(rng, w)}
def setup_inputs_ends(rng):
    d = numbers_of(rng)
    z = rng.permutation(N) % 4
    how = np.stack([rng.permutation(np.array([0, 1, 2, 2, 2, 3, 4, 5])) for r in range(N)])
    l = lists(rng, how, np.repeat(1 + z[:, None] % 2, 8, axis=1))
    x = d["x"].reshape(N, 8, 16, C, 4)
    u = d["u"].reshape(N, 128, 128, 4)
    v = d["v"]
    w = layers(rng).reshape(N, 128, 2048)
    for r in range(N):
        c = (1.0 - 2.0 * (np.argsort(gentries(l["o"][r]), axis=1) % 2)) * [2.0 ** 19, -2.0 ** -29, 0.0, 0.0][z[r]]
        if z[r] < 2:
            u[r, :, ::16] = 0
            for h in range(0, 128, 16): u[r, h:h + 16, h] = [2.0 ** 30, 2.0 ** -30][z[r]]
        else:
            k = 5.0 - 2.0 * z[r]
            c = np.full((8, C), k * 2.0 ** 19)
            u[r, :, ::16] = k * 2.0 ** 30
            v[r] = k * 2.0 ** 30
            w[r] = 2.0
        if z[r] == 1: w[r] = 0
        x[r] = c[:, None, :, None].astype(np.float32).astype(BF)
    v = (np.where(v < 0, -1.0, 1.0) * np.where(rng.permutation(N) % 2, 2.0 ** -30, 2.0 ** 30)[:, None, None]).astype(np.float32).astype(BF)
    return {"x": x.reshape(N, 128, 4 * C), "u": u.reshape(N, 128, 512), "v": v, **l, **weights(rng, w)}
def setup_inputs_spread(rng):
    d = setup_inputs(rng)
    d["x"] = big(wide(rng, N, 128, 4 * C, cols=4))
    return d
def check_inputs(d):
    b = []
    for k, lo, hi in (("x", 2.0 ** -29, 2.0 ** 19), ("u", 2.0 ** -30, 2.0 ** 30), ("v", 2.0 ** -30, 2.0 ** 30)):
        a = np.abs(d[k].astype(np.float32))
        if not (np.isfinite(a).all() and ((a == 0) | (a >= lo) & (a <= hi)).all()): b.append("a value of " + k)
    none, least, most = [emit(mx_ref.quantize(np.full((128, 16), k, np.float32).astype(BF)))[1][0, 0] for k in (0.0, 2.0 ** -30, 2.0 ** 30)]
    i = np.arange(C)
    for r in range(N):
        o, m = gentries(d["o"][r]), gentries(d["m"][r])
        if (np.sort(o, axis=1) != i).any(): b.append("o: not every item once")
        if (np.sort(m, axis=1) != i).any() or (np.take_along_axis(m, m, axis=1) != i).any() or (m[:, :B] < B).any(): b.append("m: not mates of births and deaths")
        if ((d["wc"][r] == 0x7F) | (d["wc"][r] == 0xFF)).any(): b.append("wc: a code that is no number")
        s = mx_ref.live(d["ws"][r])
        if ((s != none) & ((s < least) | (s > most))).any(): b.append("ws: a scale out of range")
        elif not (np.sum(np.abs(decode(pk(d["wc"][r], d["ws"][r])).astype(np.float64)).reshape(128, 512, 4), axis=(0, 2)) <= 1024).all(): b.append("W: a column's sum of sizes")
    return b
def of(a, i):
    return np.take_along_axis(a, i, axis=2)
def reference(x, u, v, o, m, wc, ws):
    qu = [mx_ref.quantize(u[r]) for r in range(N)]
    lay = [pk(wc[r], ws[r]) for r in range(N)]
    now = [x[r] for r in range(N)]
    at = np.stack([gentries(o[r]) for r in range(N)])
    mate = np.stack([gentries(m[r]) for r in range(N)])
    for t in range(3):
        k = t % 2
        q = [mx_ref.quantize(now[r]) for r in range(N)]
        held = [decode(q[r]).astype(BF) for r in range(N)]
        s = np.stack([mx_ref.matmul(qu[r], q[r])[::16] for r in range(N)]) + np.float32(0.0)
        place = np.argsort(at, axis=2)
        lo, hi = np.minimum(place, of(place, mate)), np.maximum(place, of(place, mate))
        a, b = at[:, :, k:C - 1:2].copy(), at[:, :, k + 1::2].copy()
        turn = (of(s, a) > of(s, b)) & (of(mate, a) != b)
        nest = (of(lo, a) < of(lo, b)) & (of(hi, b) < of(hi, a)) | (of(lo, b) < of(lo, a)) & (of(hi, a) < of(hi, b))
        switch = turn & nest & ((a < B) == (b < B))
        at2 = at.copy()
        at2[:, :, k:C - 1:2] = np.where(turn, b, a)
        at2[:, :, k + 1::2] = np.where(turn, a, b)
        c = np.zeros((N, 8, C), np.int64) + np.arange(C)
        np.put_along_axis(c, a, np.where(switch, b, a), axis=2)
        np.put_along_axis(c, b, np.where(switch, a, b), axis=2)
        mate2 = of(c, of(mate, c))
        place2 = np.argsort(at2, axis=2)
        gives = of(mate2, at2)[:, :, :B]
        sent = [mx_ref.quantize(gcols(held[r], gives[r])) for r in range(N)]
        met = np.where(place2 < B, place2, B + mate2)
        for r in range(N):
            own = gcols(held[r], mate[r])
            both = np.concatenate([decode(sent[r ^ STEP[t]]).astype(BF), held[r]], axis=1)
            z = mx_ref.quantize(((own.astype(np.float32) + gcols(both, met[r]).astype(np.float32)) * np.float32(0.5)).astype(BF))
            now[r] = tile([gpick(mx_ref.matmul(pick(lay[r], np.arange(128 * i, 128 * i + 128)), z) * np.float32(0.0078125), mate2[r]) + own[:, i::4].astype(np.float32) for i in range(4)])
        at, mate = at2, mate2
    y, om = np.zeros((N, 128, C), np.float32), np.zeros((N, 8, 2 * C), np.float32)
    oc, osc = np.zeros((N, 128, 4 * C), np.uint8), np.zeros((N, 16, C), np.uint8)
    for r in range(N):
        q = mx_ref.quantize(now[r])
        y[r] = mx_ref.matmul(mx_ref.quantize(v[r]), q)
        om[r] = np.concatenate([at[r], mate[r]], axis=1)
        oc[r], osc[r] = emit(q)
    return {"y": y, "om": om, "oc": oc, "osc": osc}

@@ -1,0 +1,407 @@
+from concourse.bass import DstId, RemoteDMATransfer
+from concourse.mybir import dt, AluOpType, ActivationFunctionType
+
+STEP = [1, 2, 4]
+C = 256
+X4 = "float8_e4m3fn_x4"
+
+SCRATCH = {
+    "XA": ("sbuf", [128, 1024], "bfloat16"), "XT": ("sbuf", [128, 1024], "bfloat16"),
+    "UT": ("sbuf", [128, 512], "bfloat16"), "VT": ("sbuf", [128, 512], "bfloat16"),
+    "ZT": ("sbuf", [128, 1024], "bfloat16"), "ET": ("sbuf", [128, 512], "bfloat16"),
+    "ONE": ("sbuf", [128, 528], "bfloat16"), "DG": ("sbuf", [128, 528], "bfloat16"),
+    "QX": ("sbuf", [128, 256], X4), "SX": ("sbuf", [128, 256], "uint8"),
+    "QZ": ("sbuf", [128, 256], X4), "SZ": ("sbuf", [128, 256], "uint8"),
+    "QU": ("sbuf", [128, 128], X4), "SU": ("sbuf", [128, 128], "uint8"),
+    "QR": ("sbuf", [128, 128], X4), "SR": ("sbuf", [128, 128], "uint8"),
+    "QV": ("sbuf", [128, 128], X4), "SV": ("sbuf", [128, 128], "uint8"),
+    "QC": ("sbuf", [128, 512], X4), "SC": ("sbuf", [128, 512], "uint8"),
+    "QW": ("sbuf", [128, 512], X4), "SW": ("sbuf", [128, 512], "uint8"),
+    "VW": ("sbuf", [128, 4 * 384], "bfloat16"),
+    "AH": ("sbuf", [128, 1024], "bfloat16"), "AF": ("sbuf", [128, 1024], "bfloat16"),
+    "GS": ("sbuf", [128, 1024], "float32"), "YS": ("sbuf", [128, 256], "float32"),
+    "OI": ("sbuf", [128, 16], "int32"), "MI": ("sbuf", [128, 16], "int32"),
+    "LU": ("sbuf", [128, 24 * 16], "uint16"), "ULI": ("sbuf", [128, 8], "int32"),
+    "QI": ("sbuf", [128, 2], "int32"), "QJ": ("sbuf", [128, 2], "int32"), "QF": ("sbuf", [128, 2], "float32"),
+    "IO": ("sbuf", [128, 256], "bfloat16"), "J16": ("sbuf", [128, 256], "bfloat16"),
+    "MK": ("sbuf", [128, 256], "bfloat16"), "RS": ("sbuf", [128, 256], "bfloat16"),
+    "DA": ("sbuf", [128, 512], "bfloat16"), "DB": ("sbuf", [128, 512], "bfloat16"),
+    "SS": ("sbuf", [128, 256], "float32"), "SP": ("sbuf", [128, 256], "float32"),
+    "D1U": ("sbuf", [128, 512], "bfloat16"), "D1M": ("sbuf", [128, 512], "bfloat16"),
+    "US": ("sbuf", [128, 512], "bfloat16"), "MS": ("sbuf", [128, 512], "bfloat16"),
+    "MM": ("sbuf", [128, 256], "bfloat16"), "MW": ("sbuf", [128, 256], "bfloat16"),
+    "GM": ("sbuf", [128, 256], "bfloat16"), "GW": ("sbuf", [128, 256], "bfloat16"),
+    "TG": ("sbuf", [128, 512], "bfloat16"),
+    "PK": ("sbuf", [128, 256], "bfloat16"), "PW": ("sbuf", [128, 256], "bfloat16"), "PF": ("sbuf", [128, 64], "float32"),
+    "GU": ("sbuf", [128, 256], "bfloat16"), "NK": ("sbuf", [128, 256], "bfloat16"), "NW": ("sbuf", [128, 256], "bfloat16"),
+    "NB": ("sbuf", [128, 16], "float32"), "M8": ("sbuf", [128, 16], "float32"), "IX": ("sbuf", [128, 16], "float32"),
+    "MR": ("sbuf", [128, 256], "bfloat16"), "OK": ("sbuf", [128, 256], "bfloat16"), "OW": ("sbuf", [128, 256], "bfloat16"),
+    "PR": ("sbuf", [128, 256], "bfloat16"), "PM": ("sbuf", [128, 256], "bfloat16"),
+    "CL": ("sbuf", [128, 256], "float32"), "ZI": ("sbuf", [128, 256], "float32"), "ZP": ("sbuf", [128, 256], "float32"),
+    "DD": ("sbuf", [128, 128], "float32"), "AB": ("sbuf", [128, 128], "float32"),
+    "NE": ("sbuf", [128, 128], "bfloat16"), "NM": ("sbuf", [128, 128], "bfloat16"), "WSG": ("sbuf", [128, 128], "bfloat16"),
+    "DO": ("sbuf", [128, 128], "bfloat16"), "DM": ("sbuf", [128, 128], "bfloat16"),
+    "OMR": ("sbuf", [128, 512], "float32"),
+}
+for _t in range(3):
+    SCRATCH["QE%d" % _t] = ("sbuf", [128, 128], X4)
+    SCRATCH["SE%d" % _t] = ("sbuf", [128, 128], "uint8")
+    SCRATCH["EL%d" % _t] = ("sbuf", [128, 128], X4)
+    SCRATCH["ES%d" % _t] = ("sbuf", [128, 128], "uint8")
+for _t in range(8):
+    SCRATCH["B%d" % _t] = ("psum", [128, 512], "float32")
+NDMA = 16
+SEMAPHORES = ["cv", "cs", "ct", "cg", "loc"] + ["arr%d" % t for t in range(3)] + ["dm%d" % t for t in range(NDMA)]
+
+
+def rank_program(g, core, T, topo):
+    rank = T.rank_of(core)
+    if rank is None:
+        return
+    ADD, SUB, MUL = AluOpType.add, AluOpType.subtract, AluOpType.mult
+    COPY, IDENT, ABS = ActivationFunctionType.Copy, ActivationFunctionType.Identity, ActivationFunctionType.Abs
+    queue = {"v": g.vector, "s": g.scalar, "t": g.tensor, "g": g, "y": g.sync}
+    total = {}
+    seen = {q: {} for q in queue}
+    acc = {}
+
+    def meet(a, b):
+        if a[0] >= b[1] or b[0] >= a[1]:
+            return False
+        return not (a[2] == b[2] and a[2] > 1 and (a[0] - b[0]) % a[2])
+
+    def norm(r):
+        return r[0], (r[1], r[2], r[3] if len(r) > 3 else 1)
+
+    def wait(q, sem, val):
+        if seen[q].get(sem, 0) < val:
+            queue[q].wait_ge(T.sem[sem], val)
+            seen[q][sem] = val
+
+    def before(q, R, W, extra=()):
+        dep = {}
+        for regs, write in ((R, False), (W, True)):
+            for r in regs:
+                name, s = norm(r)
+                excl = write or name[0] == "B" and name[1:].isdigit()
+                for (s2, w2, sem, val) in acc.get(name, []):
+                    if (excl or w2) and meet(s, s2):
+                        dep[sem] = max(dep.get(sem, 0), val)
+        for sem, val in extra:
+            dep[sem] = max(dep.get(sem, 0), val)
+        for sem in sorted(dep):
+            wait(q, sem, dep[sem])
+
+    def after(sem, val, R, W):
+        for r in W:
+            name, s = norm(r)
+            acc[name] = [e for e in acc.get(name, []) if not (s[0] <= e[0][0] and e[0][1] <= s[1] and
+                         (s[2] == 1 or s[2] == e[0][2] and (s[0] - e[0][0]) % s[2] == 0))]
+        for regs, w in ((R, False), (W, True)):
+            for r in regs:
+                name, s = norm(r)
+                acc.setdefault(name, []).append((s, w, sem, val))
+
+    def op(q, call, args, R, W, extra=(), **kw):
+        before(q, R, W, extra)
+        sem = "c" + q
+        call(*args, **kw).then_inc(T.sem[sem], 1)
+        total[sem] = total.get(sem, 0) + 1
+        after(sem, total[sem], R, W)
+
+    ndma = [0]
+
+    def dma(q, out, in_, R, W):
+        before(q, R, W)
+        sem = "dm%d" % ndma[0]
+        ndma[0] += 1
+        queue[q].dma_start(out, in_).then_inc(T.sem[sem], 16)
+        total[sem] = 16
+        after(sem, 16, R, W)
+
+    def vw(r):
+        name, (a, b, s) = norm(r)
+        return T[name][:, a:b] if s == 1 else T[name][:, a:b:s]
+
+    def tt(out, a, b, o):
+        op("v", g.vector.tensor_tensor, (vw(out), vw(a), vw(b), o), [a, b], [out])
+
+    def ttg(out, win, off, b, o):
+        op("v", g.vector.tensor_tensor, (vw(out), vw(win).indirect(vw(off)), vw(b), o), [win, off, b], [out])
+
+    def ts(out, a, s1, o1, s2=None, o2=None):
+        if o2 is None:
+            op("v", g.vector.tensor_scalar, (vw(out), vw(a), s1, None, o1), [a], [out])
+        else:
+            op("v", g.vector.tensor_scalar, (vw(out), vw(a), s1, s2, o1, o2), [a], [out])
+
+    def vcopy(out, a):
+        op("v", g.vector.tensor_copy, (vw(out), vw(a)), [a], [out])
+
+    def scopy(out, a, scale=1.0):
+        op("s", g.scalar.activation, (vw(out), vw(a), COPY), [a], [out], scale=scale)
+
+    def sgather(out, win, off, scale=1.0):
+        op("s", g.scalar.activation, (vw(out), vw(win).indirect(vw(off)), COPY), [win, off], [out], scale=scale)
+
+    def scan(out, d0, d1):
+        op("v", g.vector.tensor_tensor_scan, (vw(out), vw(d0), vw(d1), 0.0, MUL, ADD), [d0, d1], [out])
+
+    def quant(codes, plane, tile):
+        op("v", g.vector.quantize_mx, (vw(codes), vw(plane), vw(tile)), [tile], [codes, plane])
+
+    def mm(bank, n, lc, ls, rc, rs, extra=()):
+        b = ("B%d" % bank, 0, 512)
+        op("t", g.tensor.matmul_mx, (T["B%d" % bank][:, 0:n], vw(lc), vw(ls), vw(rc), vw(rs), True, True),
+           [lc, ls, rc, rs], [b], extra)
+
+    def from_bank(q, out, bank, n, scale=1.0):
+        b = ("B%d" % bank, 0, 512)
+        src = T["B%d" % bank][:, 0:n]
+        if q == "s":
+            op("s", g.scalar.activation, (vw(out), src, COPY), [b], [out], scale=scale)
+        elif scale == 1.0:
+            op("v", g.vector.tensor_copy, (vw(out), src), [b], [out])
+        else:
+            op("v", g.vector.tensor_scalar, (vw(out), src, scale, None, MUL), [b], [out])
+
+    place = {}
+
+    def L(kind, t, a=0, b=16):
+        k = place.setdefault((kind, t), len(place))
+        return ("LU", 16 * k + a, 16 * k + b)
+
+    IO, MK = ("IO", 0, 256), ("MK", 0, 256)
+
+    def wrapped(name, a=0, b=256):
+        return (name, a + 15, b, 16)
+
+    def segsum(out, src, a, b):
+        scan((out, a, b), ("RS", a, b), (src, a, b))
+
+    dma("y", T.OI[:, 0:16], T.o[:, 0:16], [], [("OI", 0, 16)])
+    dma("s", T.MI[:, 0:16], T.m[:, 0:16], [], [("MI", 0, 16)])
+    dma("y", T.XA[:, 0:1024], T.x[:, 0:1024], [], [("XA", 0, 1024)])
+    dma("s", T.UT[:, 0:512], T.u[:, 0:512], [], [("UT", 0, 512)])
+    dma("y", T.QW[:, 0:512].bitcast(dt.uint8), T.wc[:, 0:2048], [], [("QW", 0, 512)])
+    dma("y", T.SW[:, 0:512], T.ws[:, 0:512], [], [("SW", 0, 512)])
+    dma("y", T.VT[:, 0:512], T.v[:, 0:512], [], [("VT", 0, 512)])
+
+    op("v", g.vector.memset, (T.ONE[:, 0:528], 1.0), [], [("ONE", 0, 528)])
+    op("g", g.iota, (T.IO[:, 0:256], [[1, 256]], 0, 0), [], [IO], allow_small_or_imprecise_dtypes=True)
+    op("g", g.iota, (T.J16[:, 0:256], [[0, 16], [1, 16]], 0, 0), [], [("J16", 0, 256)], allow_small_or_imprecise_dtypes=True)
+    op("g", g.iota, (T.QI[:, 0:2], [[0, 2]], 0, 1), [], [("QI", 0, 2)])
+    op("g", g.iota, (T.ULI[:, 0:8], [[16, 8]], 0, 0), [], [("ULI", 0, 8)])
+    op("g", g.affine_select, (T.DG[:, 0:528], T.ONE[:, 0:528], [[-1, 528]], AluOpType.is_equal, 0.0, 3, 4),
+       [("ONE", 0, 528)], [("DG", 0, 528)])
+    ts(("QJ", 0, 2), ("QI", 0, 2), 15, AluOpType.bitwise_and)
+    vcopy(("QF", 0, 2), ("QJ", 0, 2))
+    op("v", g.vector.tensor_scalar, (T.MK[:, 0:256], T.J16[:, 0:256], T.QF[:, 0:1], None, AluOpType.is_equal),
+       [("J16", 0, 256), ("QF", 0, 2)], [MK])
+    ts(("RS", 0, 256), ("J16", 0, 256), 0.0, AluOpType.not_equal)
+    vcopy(L("u", 0, 0, 8), ("ULI", 0, 8))
+    for name, base in (("DA", 0), ("DB", 2)):
+        for k, c in ((0, 0.0), (2, -1.0), (3, 1.0)):
+            a = (base + k) % 4
+            op("v", g.vector.memset, (T[name][:, a:512:4], c), [], [(name, a, 512, 4)])
+    op("v", g.vector.memset, (T.TG[:, 256:512], 0.0), [], [("TG", 256, 512)])
+
+    vcopy(L("o", 0), ("OI", 0, 16))
+    vcopy(L("m", 0), ("MI", 0, 16))
+    PR = ("PR", 0, 256)
+    op("v", g.vector.tensor_copy, (T.PR[:, 0:256].indirect(vw(L("o", 0))), T.IO[:, 0:256]), [IO, L("o", 0)], [PR])
+    sgather(("PM", 0, 256), PR, L("m", 0))
+    quant(("QX", 0, 256), ("SX", 0, 256), ("XA", 0, 1024))
+    quant(("QU", 0, 128), ("SU", 0, 128), ("UT", 0, 512))
+    ul = L("u", 0, 0, 8)
+    op("v", g.vector.tensor_copy, (T.QR[:, 0:128].bitcast(dt.uint32), T.QU[:, 0:128].bitcast(dt.uint32).indirect(vw(ul))),
+       [("QU", 0, 128), ul], [("QR", 0, 128)])
+    op("v", g.vector.tensor_copy, (T.SR[:, 0:128], T.SU[:, 0:128].indirect(vw(ul))),
+       [("SU", 0, 128), ul], [("SR", 0, 128)])
+    for b in range(4):
+        quant(("QC", 128 * b, 128 * b + 128), ("SC", 128 * b, 128 * b + 128), ("DG", 3 - b, 515 - b))
+    tt(("CL", 0, 256), ("PM", 0, 256), PR, AluOpType.is_gt)
+    ts(("CL", 0, 128), ("CL", 0, 128), 1536.0, MUL)
+    ts(("CL", 128, 256), ("CL", 128, 256), 512.0, MUL, 512.0, ADD)
+
+    def couples(t):
+        return (2, 127) if t % 2 else (0, 128)
+
+    def rows(t):
+        sgather(("D1U", 1, 512, 2), IO, L("o", t))
+        sgather(("D1M", 1, 512, 2), ("PM", 0, 256), L("o", t))
+        base, nc = couples(t)
+        end = base + 4 * nc
+        for n in ("D1U", "D1M"):
+            scopy((n, base + 2, end, 4), (n, base + 1, end, 4))
+        if t % 2:
+            scopy(("US", 1, 512, 510), ("D1U", 1, 512, 510))
+            scopy(("MS", 1, 512, 510), ("D1M", 1, 512, 510))
+
+    def weights1(t):
+        k0 = t % 2
+        base, nc = couples(t)
+        e = k0 + 2 * nc
+        sgather(("ZP", 0, 256), ("ZI", 0, 256), L("o", t))
+        tt(("DD", 0, nc), ("ZP", k0, e, 2), ("ZP", k0 + 1, min(e + 1, 256), 2), SUB)
+        ts(("NM", 0, nc), ("DD", 0, nc), 1025.0, AluOpType.not_equal)
+        op("s", g.scalar.activation, (T.AB[:, 0:nc], T.DD[:, 0:nc], ABS), [("DD", 0, nc)], [("AB", 0, nc)], bias=-128.0)
+        ts(("NE", 0, nc), ("AB", 0, nc), 127.5, AluOpType.is_lt)
+        tt(("WSG", 0, nc), ("NM", 0, nc), ("NE", 0, nc), SUB)
+
+    def weights2(t):
+        base, nc = couples(t)
+        end = base + 4 * nc
+        tt(("DO", 0, nc), ("D1U", base + 3, end, 4), ("D1U", base + 1, end, 4), SUB)
+        tt(("DM", 0, nc), ("D1M", base + 3, end, 4), ("D1M", base + 1, end, 4), SUB)
+
+    def weights3(t):
+        base, nc = couples(t)
+        end = base + 4 * nc
+        tt(("D1U", base, end, 4), ("NE", 0, nc), ("DO", 0, nc), MUL)
+        tt(("D1M", base, end, 4), ("WSG", 0, nc), ("DM", 0, nc), MUL)
+
+    def zmake(t):
+        ttg(("ZI", 0, 256), PR, L("m", t), ("CL", 0, 256), ADD)
+
+    zmake(0)
+    rows(0)
+    weights1(0)
+    weights2(0)
+    weights3(0)
+    tt(("PK", 0, 256), PR, MK, MUL)
+    segsum("PW", "PK", 0, 256)
+    vcopy(("PF", 0, 16), wrapped("PW"))
+    vcopy(L("p", 0), wrapped("PW"))
+
+    for t in range(3):
+        k0 = t % 2
+        base, nc = couples(t)
+        end = base + 4 * nc
+        e = k0 + 2 * nc
+        last = t == 2
+        D0 = "DB" if t % 2 else "DA"
+        partner = T.cores[rank ^ STEP[t]]
+        mm(7, 256, ("QR", 0, 128), ("SR", 0, 128), ("QX", 0, 256), ("SX", 0, 256))
+        for b in range(4):
+            mm(b, 256, ("QC", 128 * b, 128 * b + 128), ("SC", 128 * b, 128 * b + 128), ("QX", 0, 256), ("SX", 0, 256))
+        from_bank("v", ("SS", 0, 256), 7, 256)
+        op("v", g.vector.tensor_copy, (T.SP[:, 0:128], T.SS[:, 0:256].indirect(vw(L("o", t, 0, 8)))),
+           [("SS", 0, 256), L("o", t, 0, 8)], [("SP", 0, 128)])
+        sgather(("SP", 128, 256), ("SS", 0, 256), L("o", t, 8, 16))
+        for b in range(4):
+            from_bank("s", ("VW", 384 * b + 128, 384 * b + 384), b, 256, 0.5)
+        TR = (D0, base + 1, end, 4)
+        tt(TR, ("SP", k0, e, 2), ("SP", k0 + 1, min(e + 1, 256), 2), AluOpType.is_gt)
+        h = base + 4 * 64
+        scan(("MS", base, h), (D0, base, h), ("D1M", base, h))
+        scan(("US", base, end), (D0, base, end), ("D1U", base, end))
+
+        def mates_places(a, b):
+            tt(("MM", a, b), ("MS", 2 * a + 1, 2 * b, 2), ("MK", a, b), MUL)
+            segsum("MW", "MM", a, b)
+            ts(L("M", t, a // 16, b // 16), wrapped("MW", a, b), 2.0, MUL, 1.0, ADD)
+
+        def gives(a, b):
+            ttg(("GM", a, b), ("US", 0, 512), L("M", t, a // 16, b // 16), ("MK", a, b), MUL)
+            segsum("GW", "GM", a, b)
+            vcopy(L("g", t, a // 16, b // 16), wrapped("GW", a, b))
+
+        mates_places(0, 128)
+        gives(0, 128)
+        for b in range(2):
+            op("v", g.vector.tensor_scalar, (T.ET[:, b:512:4], T.VW[:, 384 * b + 128:384 * b + 384].indirect(vw(L("g", t, 0, 8))),
+               2.0, None, MUL), [("VW", 384 * b + 128, 384 * b + 384), L("g", t, 0, 8)], [("ET", b, 512, 4)])
+        for b in range(2, 4):
+            sgather(("ET", b, 512, 4), ("VW", 384 * b + 128, 384 * b + 384), L("g", t, 0, 8), 2.0)
+        QE, SE = ("QE%d" % t, 0, 128), ("SE%d" % t, 0, 128)
+        quant(QE, SE, ("ET", 0, 512))
+        before("g", [QE, SE], [])
+        rid, pid = topo.addr(partner, core)
+        mask = topo.mask(core, partner)
+        g.remote_dma(T["EL%d" % t][:, 0:128].bitcast(dt.uint8), T["QE%d" % t][:, 0:128].bitcast(dt.uint8),
+                     T.sem["arr%d" % t], T.sem["loc"], pid, rid, mask)
+        g.remote_dma(T["ES%d" % t][:, 0:128], T["SE%d" % t][:, 0:128],
+                     T.sem["arr%d" % t], T.sem["loc"], pid, rid, mask)
+        lanes = 2 * len(topo.engines(core, partner))
+        total["loc"] = total.get("loc", 0) + lanes
+
+        tg = 256 * k0
+        tt(("TG", tg + k0, tg + e, 2), TR, ("NM", 0, nc), MUL)
+        scopy(("TG", tg + k0 + 1, tg + min(e + 1, 256), 2), ("TG", tg + k0, tg + e, 2), -1.0)
+        if base + 4 * nc > h:
+            scan(("MS", h, end), (D0, h, end), ("D1M", h, end))
+        mates_places(128, 256)
+        sgather(("GU", 0, 256), ("US", 0, 512), L("M", t))
+        ttg(("PK", 0, 256), ("TG", tg, tg + 256), L("p", t), MK, MUL)
+        segsum("PW", "PK", 0, 256)
+        pf, pf2 = ("PF", 16 * t, 16 * t + 16), ("PF", 16 * t + 16, 16 * t + 32)
+        tt(pf2, pf, wrapped("PW"), ADD)
+        vcopy(L("p", t + 1), pf2)
+        if not last:
+            sgather(PR, IO, L("p", t + 1))
+        ttg(("NK", 0, 256), ("GU", 0, 256), L("p", t + 1), MK, MUL)
+        segsum("NW", "NK", 0, 256)
+        vcopy(L("m", t + 1), wrapped("NW"))
+        sgather(("MR", 0, 256), IO, L("m", t + 1))
+        ts(("M8", 0, 16), wrapped("NW"), 128.0, ADD)
+        ts(("NB", 0, 16), pf2, 128.0, AluOpType.is_ge)
+        tt(("M8", 0, 16), ("M8", 0, 16), pf2, SUB)
+        gives(128, 256)
+        tt(("M8", 0, 16), ("M8", 0, 16), ("NB", 0, 16), MUL)
+        for b in range(2):
+            sgather(("AH", 256 * b, 256 * b + 256), ("VW", 384 * b + 128, 384 * b + 384), L("m", t))
+        tt(("IX", 0, 16), ("M8", 0, 16), pf2, ADD)
+        vcopy(L("i", t), ("IX", 0, 16))
+        ttg(("OK", 0, 256), ("MR", 0, 256), L("g", t), MK, MUL)
+        segsum("OW", "OK", 0, 256)
+        vcopy(L("o", t + 1), wrapped("OW"))
+        if not last:
+            zmake(t + 1)
+            sgather(("PM", 0, 256), PR, L("m", t + 1))
+        for b in range(2, 4):
+            sgather(("AH", 256 * b, 256 * b + 256), ("VW", 384 * b + 128, 384 * b + 384), L("m", t))
+        if not last:
+            weights1(t + 1)
+        else:
+            sgather(("OMR", 0, 256), IO, L("o", 3))
+            sgather(("OMR", 256, 512), IO, L("m", 3))
+            dma("y", T.om[:, 0:512], T.OMR[0:128:16, 0:512], [("OMR", 0, 512)], [])
+            quant(("QV", 0, 128), ("SV", 0, 128), ("VT", 0, 512))
+        ED = [4, 5, 6, 0]
+        for b in range(4):
+            mm(ED[b], 128, ("QC", 128 * b, 128 * b + 128), ("SC", 128 * b, 128 * b + 128), ("EL%d" % t, 0, 128), ("ES%d" % t, 0, 128),
+               [("arr%d" % t, lanes)])
+        for b in range(4):
+            from_bank("s", ("VW", 384 * b, 384 * b + 128), ED[b], 128, 0.5)
+        GB = [[1, 2, 3, 4], [5, 6, 0, 1]]
+        for hh in range(2):
+            for b in range(4):
+                c0 = 256 * b + 128 * hh
+                ttg(("ZT", 512 * hh + b, 512 * hh + 512, 4), ("VW", 384 * b, 384 * b + 384), L("i", t, 8 * hh, 8 * hh + 8),
+                    ("AH", c0, c0 + 128), ADD)
+            z = (128 * hh, 128 * hh + 128)
+            quant(("QZ",) + z, ("SZ",) + z, ("ZT", 512 * hh, 512 * hh + 512))
+            for b in range(4):
+                mm(GB[hh][b], 128, ("QW", 128 * b, 128 * b + 128), ("SW", 128 * b, 128 * b + 128), ("QZ",) + z, ("SZ",) + z)
+            if hh == 0:
+                scopy(("AF", 0, 1024), ("AH", 0, 1024), 2.0)
+            for b in range(4):
+                from_bank("s", ("GS", 256 * b + 128 * hh, 256 * b + 128 * hh + 128), GB[hh][b], 128, 0.0078125)
+        if not last:
+            rows(t + 1)
+            weights2(t + 1)
+        for b in range(4):
+            ttg(("XT", b, 1024, 4), ("GS", 256 * b, 256 * b + 256), L("m", t + 1), ("AF", 256 * b, 256 * b + 256), ADD)
+        quant(("QX", 0, 256), ("SX", 0, 256), ("XT", 0, 1024))
+        if not last:
+            weights3(t + 1)
+
+    mm(7, 256, ("QV", 0, 128), ("SV", 0, 128), ("QX", 0, 256), ("SX", 0, 256))
+    from_bank("v", ("YS", 0, 256), 7, 256)
+    dma("y", T.oc[:, 0:1024], T.QX[:, 0:256].bitcast(dt.uint8), [("QX", 0, 256)], [])
+    for k in range(4):
+        dma("s" if k % 2 else "y", T.osc[4 * k:4 * k + 4, 0:256], T.SX[32 * k:32 * k + 4, 0:256], [("SX", 0, 256)], [])
+    dma("y", T.y[:, 0:256], T.YS[:, 0:256], [("YS", 0, 256)], [])
+    for sem in sorted(total):
+        wait("g", sem, total[sem])

@@ -34,10 +34,11 @@ SCRATCH = {
     "TG": ("sbuf", [128, 512], "bfloat16"),
     "PK": ("sbuf", [128, 256], "bfloat16"), "PW": ("sbuf", [128, 256], "bfloat16"), "PF": ("sbuf", [128, 64], "float32"),
     "GU": ("sbuf", [128, 256], "bfloat16"), "NK": ("sbuf", [128, 256], "bfloat16"), "NW": ("sbuf", [128, 256], "bfloat16"),
-    "NB": ("sbuf", [128, 16], "float32"), "M8": ("sbuf", [128, 16], "float32"), "IX": ("sbuf", [128, 16], "float32"),
+    "NB": ("sbuf", [128, 16], "float32"), "NZ": ("sbuf", [128, 16], "float32"), "IX": ("sbuf", [128, 16], "float32"),
     "MR": ("sbuf", [128, 256], "bfloat16"), "OK": ("sbuf", [128, 256], "bfloat16"), "OW": ("sbuf", [128, 256], "bfloat16"),
-    "PR": ("sbuf", [128, 256], "bfloat16"), "PM": ("sbuf", [128, 256], "bfloat16"),
-    "CL": ("sbuf", [128, 256], "float32"), "ZI": ("sbuf", [128, 256], "float32"), "ZP": ("sbuf", [128, 256], "float32"),
+    "PR": ("sbuf", [128, 256], "bfloat16"), "PM": ("sbuf", [128, 256], "bfloat16"), "SD": ("sbuf", [128, 256], "bfloat16"),
+    "CL": ("sbuf", [128, 256], "float32"), "CM": ("sbuf", [128, 256], "float32"),
+    "ZI": ("sbuf", [128, 256], "float32"), "ZP": ("sbuf", [128, 256], "float32"),
     "DD": ("sbuf", [128, 128], "float32"), "AB": ("sbuf", [128, 128], "float32"),
     "NE": ("sbuf", [128, 128], "bfloat16"), "NM": ("sbuf", [128, 128], "bfloat16"), "WSG": ("sbuf", [128, 128], "bfloat16"),
     "DO": ("sbuf", [128, 128], "bfloat16"), "DM": ("sbuf", [128, 128], "bfloat16"),
@@ -58,8 +59,8 @@ def rank_program(g, core, T, topo):
     rank = T.rank_of(core)
     if rank is None:
         return
-    ADD, SUB, MUL = AluOpType.add, AluOpType.subtract, AluOpType.mult
-    COPY, IDENT, ABS = ActivationFunctionType.Copy, ActivationFunctionType.Identity, ActivationFunctionType.Abs
+    ADD, SUB, MUL, MAX = AluOpType.add, AluOpType.subtract, AluOpType.mult, AluOpType.max
+    COPY, ABS = ActivationFunctionType.Copy, ActivationFunctionType.Abs
     queue = {"v": g.vector, "s": g.scalar, "t": g.tensor, "g": g, "y": g.sync}
     total = {}
     seen = {q: {} for q in queue}
@@ -171,7 +172,7 @@ def rank_program(g, core, T, topo):
         k = place.setdefault((kind, t), len(place))
         return ("LU", 16 * k + a, 16 * k + b)
 
-    IO, MK = ("IO", 0, 256), ("MK", 0, 256)
+    IO, MK, PR = ("IO", 0, 256), ("MK", 0, 256), ("PR", 0, 256)
 
     def wrapped(name, a=0, b=256):
         return (name, a + 15, b, 16)
@@ -206,73 +207,70 @@ def rank_program(g, core, T, topo):
             op("v", g.vector.memset, (T[name][:, a:512:4], c), [], [(name, a, 512, 4)])
     op("v", g.vector.memset, (T.TG[:, 256:512], 0.0), [], [("TG", 256, 512)])
 
+    def couples(t):
+        return (2, 127) if t % 2 else (0, 128)
+
+    def row(name, keep, win, off, t):
+        base, nc = couples(t)
+        end = base + 4 * nc
+        sgather((name, 1, 512, 2), win, off)
+        scopy((name, base + 2, end, 4), (name, base + 1, end, 4))
+        if t % 2:
+            scopy((keep, 1, 512, 510), (name, 1, 512, 510))
+
+    def zdiff(t):
+        k0 = t % 2
+        nc = couples(t)[1]
+        tt(("DD", 0, nc), ("ZP", k0, k0 + 2 * nc, 2), ("ZP", k0 + 1, min(k0 + 2 * nc + 1, 256), 2), SUB)
+        op("s", g.scalar.activation, (T.AB[:, 0:nc], T.DD[:, 0:nc], ABS), [("DD", 0, nc)], [("AB", 0, nc)], bias=-128.0)
+
+    def kinds(t):
+        nc = couples(t)[1]
+        ts(("NM", 0, nc), ("DD", 0, nc), 256.0, AluOpType.not_equal)
+        ts(("NE", 0, nc), ("AB", 0, nc), 127.5, AluOpType.is_lt)
+        ts(("WSG", 0, nc), ("AB", 0, nc), 128.5, AluOpType.is_gt)
+
+    def step_o(t):
+        base, nc = couples(t)
+        end = base + 4 * nc
+        tt(("DO", 0, nc), ("D1U", base + 3, end, 4), ("D1U", base + 1, end, 4), SUB)
+
+    def step_m(t):
+        base, nc = couples(t)
+        end = base + 4 * nc
+        tt(("DM", 0, nc), ("D1M", base + 3, end, 4), ("D1M", base + 1, end, 4), SUB)
+
+    def weigh(t):
+        base, nc = couples(t)
+        end = base + 4 * nc
+        tt(("D1M", base, end, 4), ("WSG", 0, nc), ("DM", 0, nc), MUL)
+        tt(("D1U", base, end, 4), ("NE", 0, nc), ("DO", 0, nc), MUL)
+
     vcopy(L("o", 0), ("OI", 0, 16))
     vcopy(L("m", 0), ("MI", 0, 16))
-    PR = ("PR", 0, 256)
     op("v", g.vector.tensor_copy, (T.PR[:, 0:256].indirect(vw(L("o", 0))), T.IO[:, 0:256]), [IO, L("o", 0)], [PR])
     sgather(("PM", 0, 256), PR, L("m", 0))
     quant(("QX", 0, 256), ("SX", 0, 256), ("XA", 0, 1024))
     quant(("QU", 0, 128), ("SU", 0, 128), ("UT", 0, 512))
+    tt(("SD", 0, 256), ("PM", 0, 256), PR, AluOpType.is_gt)
     ul = L("u", 0, 0, 8)
+    op("s", g.scalar.activation, (T.SR[:, 0:128], T.SU[:, 0:128].indirect(vw(ul)), COPY),
+       [("SU", 0, 128), ul], [("SR", 0, 128)])
+    row("D1U", "US", IO, L("o", 0), 0)
+    ts(("CL", 0, 128), ("SD", 0, 128), 1279.0, MUL)
+    ts(("CL", 128, 256), ("SD", 128, 256), -769.0, MUL, 1024.0, ADD)
+    ttg(("ZI", 0, 256), PR, L("m", 0), ("CL", 0, 256), ADD)
+    sgather(("ZP", 0, 256), ("ZI", 0, 256), L("o", 0))
+    row("D1M", "MS", ("PM", 0, 256), L("o", 0), 0)
     op("v", g.vector.tensor_copy, (T.QR[:, 0:128].bitcast(dt.uint32), T.QU[:, 0:128].bitcast(dt.uint32).indirect(vw(ul))),
        [("QU", 0, 128), ul], [("QR", 0, 128)])
-    op("v", g.vector.tensor_copy, (T.SR[:, 0:128], T.SU[:, 0:128].indirect(vw(ul))),
-       [("SU", 0, 128), ul], [("SR", 0, 128)])
     for b in range(4):
         quant(("QC", 128 * b, 128 * b + 128), ("SC", 128 * b, 128 * b + 128), ("DG", 3 - b, 515 - b))
-    tt(("CL", 0, 256), ("PM", 0, 256), PR, AluOpType.is_gt)
-    ts(("CL", 0, 128), ("CL", 0, 128), 1536.0, MUL)
-    ts(("CL", 128, 256), ("CL", 128, 256), 512.0, MUL, 512.0, ADD)
-
-    def couples(t):
-        return (2, 127) if t % 2 else (0, 128)
-
-    def rows(t):
-        sgather(("D1U", 1, 512, 2), IO, L("o", t))
-        sgather(("D1M", 1, 512, 2), ("PM", 0, 256), L("o", t))
-        base, nc = couples(t)
-        end = base + 4 * nc
-        for n in ("D1U", "D1M"):
-            scopy((n, base + 2, end, 4), (n, base + 1, end, 4))
-        if t % 2:
-            scopy(("US", 1, 512, 510), ("D1U", 1, 512, 510))
-            scopy(("MS", 1, 512, 510), ("D1M", 1, 512, 510))
-
-    def weights1(t):
-        k0 = t % 2
-        base, nc = couples(t)
-        e = k0 + 2 * nc
-        sgather(("ZP", 0, 256), ("ZI", 0, 256), L("o", t))
-        tt(("DD", 0, nc), ("ZP", k0, e, 2), ("ZP", k0 + 1, min(e + 1, 256), 2), SUB)
-        ts(("NM", 0, nc), ("DD", 0, nc), 1025.0, AluOpType.not_equal)
-        op("s", g.scalar.activation, (T.AB[:, 0:nc], T.DD[:, 0:nc], ABS), [("DD", 0, nc)], [("AB", 0, nc)], bias=-128.0)
-        ts(("NE", 0, nc), ("AB", 0, nc), 127.5, AluOpType.is_lt)
-        tt(("WSG", 0, nc), ("NM", 0, nc), ("NE", 0, nc), SUB)
-
-    def weights2(t):
-        base, nc = couples(t)
-        end = base + 4 * nc
-        tt(("DO", 0, nc), ("D1U", base + 3, end, 4), ("D1U", base + 1, end, 4), SUB)
-        tt(("DM", 0, nc), ("D1M", base + 3, end, 4), ("D1M", base + 1, end, 4), SUB)
-
-    def weights3(t):
-        base, nc = couples(t)
-        end = base + 4 * nc
-        tt(("D1U", base, end, 4), ("NE", 0, nc), ("DO", 0, nc), MUL)
-        tt(("D1M", base, end, 4), ("WSG", 0, nc), ("DM", 0, nc), MUL)
-
-    def zmake(t):
-        ttg(("ZI", 0, 256), PR, L("m", t), ("CL", 0, 256), ADD)
-
-    zmake(0)
-    rows(0)
-    weights1(0)
-    weights2(0)
-    weights3(0)
-    tt(("PK", 0, 256), PR, MK, MUL)
-    segsum("PW", "PK", 0, 256)
-    vcopy(("PF", 0, 16), wrapped("PW"))
-    vcopy(L("p", 0), wrapped("PW"))
+    zdiff(0)
+    step_o(0)
+    kinds(0)
+    step_m(0)
+    weigh(0)
 
     for t in range(3):
         k0 = t % 2
@@ -282,15 +280,26 @@ def rank_program(g, core, T, topo):
         last = t == 2
         D0 = "DB" if t % 2 else "DA"
         partner = T.cores[rank ^ STEP[t]]
+
+        def plane_h(b):
+            return ("VW", 384 * b, 384 * b + 256)
+
+        def a_half(b):
+            sgather(("AH", 256 * b, 256 * b + 256), plane_h(b), L("m", t))
+
+        def a_full(b):
+            scopy(("AF", 256 * b, 256 * b + 256), ("AH", 256 * b, 256 * b + 256), 2.0)
+
         mm(7, 256, ("QR", 0, 128), ("SR", 0, 128), ("QX", 0, 256), ("SX", 0, 256))
         for b in range(4):
             mm(b, 256, ("QC", 128 * b, 128 * b + 128), ("SC", 128 * b, 128 * b + 128), ("QX", 0, 256), ("SX", 0, 256))
-        from_bank("v", ("SS", 0, 256), 7, 256)
+        from_bank("s", ("SS", 0, 256), 7, 256)
         op("v", g.vector.tensor_copy, (T.SP[:, 0:128], T.SS[:, 0:256].indirect(vw(L("o", t, 0, 8)))),
            [("SS", 0, 256), L("o", t, 0, 8)], [("SP", 0, 128)])
         sgather(("SP", 128, 256), ("SS", 0, 256), L("o", t, 8, 16))
         for b in range(4):
-            from_bank("s", ("VW", 384 * b + 128, 384 * b + 384), b, 256, 0.5)
+            from_bank("s", plane_h(b), b, 256, 0.5)
+        a_half(0)
         TR = (D0, base + 1, end, 4)
         tt(TR, ("SP", k0, e, 2), ("SP", k0 + 1, min(e + 1, 256), 2), AluOpType.is_gt)
         h = base + 4 * 64
@@ -310,10 +319,10 @@ def rank_program(g, core, T, topo):
         mates_places(0, 128)
         gives(0, 128)
         for b in range(2):
-            op("v", g.vector.tensor_scalar, (T.ET[:, b:512:4], T.VW[:, 384 * b + 128:384 * b + 384].indirect(vw(L("g", t, 0, 8))),
-               2.0, None, MUL), [("VW", 384 * b + 128, 384 * b + 384), L("g", t, 0, 8)], [("ET", b, 512, 4)])
+            op("v", g.vector.tensor_scalar, (T.ET[:, b:512:4], vw(plane_h(b)).indirect(vw(L("g", t, 0, 8))), 2.0, None, MUL),
+               [plane_h(b), L("g", t, 0, 8)], [("ET", b, 512, 4)])
         for b in range(2, 4):
-            sgather(("ET", b, 512, 4), ("VW", 384 * b + 128, 384 * b + 384), L("g", t, 0, 8), 2.0)
+            sgather(("ET", b, 512, 4), plane_h(b), L("g", t, 0, 8), 2.0)
         QE, SE = ("QE%d" % t, 0, 128), ("SE%d" % t, 0, 128)
         quant(QE, SE, ("ET", 0, 512))
         before("g", [QE, SE], [])
@@ -329,51 +338,59 @@ def rank_program(g, core, T, topo):
         tg = 256 * k0
         tt(("TG", tg + k0, tg + e, 2), TR, ("NM", 0, nc), MUL)
         scopy(("TG", tg + k0 + 1, tg + min(e + 1, 256), 2), ("TG", tg + k0, tg + e, 2), -1.0)
-        if base + 4 * nc > h:
-            scan(("MS", h, end), (D0, h, end), ("D1M", h, end))
+        a_half(1)
+        scan(("MS", h, end), (D0, h, end), ("D1M", h, end))
+        if t == 0:
+            tt(("NK", 0, 256), PR, MK, MUL)
         mates_places(128, 256)
+        if t == 0:
+            segsum("NW", "NK", 0, 256)
+            vcopy(L("p", 0), wrapped("NW"))
+            ts(("PF", 0, 16), wrapped("NW"), 256.0, ADD)
         sgather(("GU", 0, 256), ("US", 0, 512), L("M", t))
         ttg(("PK", 0, 256), ("TG", tg, tg + 256), L("p", t), MK, MUL)
         segsum("PW", "PK", 0, 256)
+        if t == 0:
+            ts(("CM", 0, 128), ("SD", 0, 128), 769.0, MUL, 255.0, ADD)
+            ts(("CM", 128, 256), ("SD", 128, 256), -1279.0, MUL, 1279.0, ADD)
         pf, pf2 = ("PF", 16 * t, 16 * t + 16), ("PF", 16 * t + 16, 16 * t + 32)
         tt(pf2, pf, wrapped("PW"), ADD)
-        vcopy(L("p", t + 1), pf2)
+        ts(L("p", t + 1), pf2, -256.0, ADD)
+        ts(("NB", 0, 16), pf2, 384.0, AluOpType.is_ge, -1000.0, MUL)
+        ttg(("NK", 0, 256), ("GU", 0, 256), L("p", t + 1), MK, MUL)
         if not last:
             sgather(PR, IO, L("p", t + 1))
-        ttg(("NK", 0, 256), ("GU", 0, 256), L("p", t + 1), MK, MUL)
         segsum("NW", "NK", 0, 256)
+        tt(("NZ", 0, 16), ("NB", 0, 16), pf2, ADD)
         vcopy(L("m", t + 1), wrapped("NW"))
         sgather(("MR", 0, 256), IO, L("m", t + 1))
-        ts(("M8", 0, 16), wrapped("NW"), 128.0, ADD)
-        ts(("NB", 0, 16), pf2, 128.0, AluOpType.is_ge)
-        tt(("M8", 0, 16), ("M8", 0, 16), pf2, SUB)
+        if not last:
+            ttg(("ZI", 0, 256), IO, L("p", t + 1), ("CM", 0, 256), ADD)
+        tt(("IX", 0, 16), ("NZ", 0, 16), wrapped("NW"), MAX)
         gives(128, 256)
-        tt(("M8", 0, 16), ("M8", 0, 16), ("NB", 0, 16), MUL)
-        for b in range(2):
-            sgather(("AH", 256 * b, 256 * b + 256), ("VW", 384 * b + 128, 384 * b + 384), L("m", t))
-        tt(("IX", 0, 16), ("M8", 0, 16), pf2, ADD)
         vcopy(L("i", t), ("IX", 0, 16))
+        if not last:
+            sgather(("ZP", 0, 256), ("ZI", 0, 256), L("g", t))
         ttg(("OK", 0, 256), ("MR", 0, 256), L("g", t), MK, MUL)
+        a_half(2)
         segsum("OW", "OK", 0, 256)
+        if not last:
+            zdiff(t + 1)
         vcopy(L("o", t + 1), wrapped("OW"))
         if not last:
-            zmake(t + 1)
-            sgather(("PM", 0, 256), PR, L("m", t + 1))
-        for b in range(2, 4):
-            sgather(("AH", 256 * b, 256 * b + 256), ("VW", 384 * b + 128, 384 * b + 384), L("m", t))
-        if not last:
-            weights1(t + 1)
+            kinds(t + 1)
         else:
-            sgather(("OMR", 0, 256), IO, L("o", 3))
-            sgather(("OMR", 256, 512), IO, L("m", 3))
-            dma("y", T.om[:, 0:512], T.OMR[0:128:16, 0:512], [("OMR", 0, 512)], [])
             quant(("QV", 0, 128), ("SV", 0, 128), ("VT", 0, 512))
+        a_half(3)
         ED = [4, 5, 6, 0]
         for b in range(4):
             mm(ED[b], 128, ("QC", 128 * b, 128 * b + 128), ("SC", 128 * b, 128 * b + 128), ("EL%d" % t, 0, 128), ("ES%d" % t, 0, 128),
                [("arr%d" % t, lanes)])
         for b in range(4):
-            from_bank("s", ("VW", 384 * b, 384 * b + 128), ED[b], 128, 0.5)
+            from_bank("vvss"[b], ("VW", 384 * b + 256, 384 * b + 384), ED[b], 128, 0.5)
+        if not last:
+            row("D1U", "US", IO, L("o", t + 1), t + 1)
+            row("D1M", "MS", PR, L("g", t), t + 1)
         GB = [[1, 2, 3, 4], [5, 6, 0, 1]]
         for hh in range(2):
             for b in range(4):
@@ -384,18 +401,25 @@ def rank_program(g, core, T, topo):
             quant(("QZ",) + z, ("SZ",) + z, ("ZT", 512 * hh, 512 * hh + 512))
             for b in range(4):
                 mm(GB[hh][b], 128, ("QW", 128 * b, 128 * b + 128), ("SW", 128 * b, 128 * b + 128), ("QZ",) + z, ("SZ",) + z)
-            if hh == 0:
-                scopy(("AF", 0, 1024), ("AH", 0, 1024), 2.0)
             for b in range(4):
                 from_bank("s", ("GS", 256 * b + 128 * hh, 256 * b + 128 * hh + 128), GB[hh][b], 128, 0.0078125)
+                if hh == 1 and b < 2:
+                    a_full(b + 2)
+            if hh == 0:
+                a_full(0)
+                a_full(1)
         if not last:
-            rows(t + 1)
-            weights2(t + 1)
+            step_o(t + 1)
+            step_m(t + 1)
         for b in range(4):
             ttg(("XT", b, 1024, 4), ("GS", 256 * b, 256 * b + 256), L("m", t + 1), ("AF", 256 * b, 256 * b + 256), ADD)
         quant(("QX", 0, 256), ("SX", 0, 256), ("XT", 0, 1024))
         if not last:
-            weights3(t + 1)
+            weigh(t + 1)
+        else:
+            sgather(("OMR", 0, 256), IO, L("o", 3))
+            sgather(("OMR", 256, 512), IO, L("m", 3))
+            dma("y", T.om[:, 0:512], T.OMR[0:128:16, 0:512], [("OMR", 0, 512)], [])
 
     mm(7, 256, ("QV", 0, 128), ("SV", 0, 128), ("QX", 0, 256), ("SX", 0, 256))
     from_bank("v", ("YS", 0, 256), 7, 256)

@@ -189,8 +189,10 @@ def rank_program(g, core, T, topo):
     dma("y", T.VT[:, 0:512], T.v[:, 0:512], [], [("VT", 0, 512)])
 
     op("v", g.vector.memset, (T.ONE[:, 0:528], 1.0), [], [("ONE", 0, 528)])
-    op("g", g.iota, (T.IO[:, 0:256], [[1, 256]], 0, 0), [], [IO], allow_small_or_imprecise_dtypes=True)
-    op("g", g.iota, (T.J16[:, 0:256], [[0, 16], [1, 16]], 0, 0), [], [("J16", 0, 256)], allow_small_or_imprecise_dtypes=True)
+    op("v", g.vector.memset, (T.RS[:, 0:256], 1.0), [], [("RS", 0, 256)])
+    op("v", g.vector.memset, (T.RS[:, 0:256:16], 0.0), [], [("RS", 0, 256, 16)])
+    op("v", g.vector.tensor_tensor_scan, (T.IO[:, 0:256], T.ONE[:, 0:256], T.ONE[:, 0:256], -1.0, MUL, ADD), [("ONE", 0, 256)], [IO])
+    scan(("J16", 0, 256), ("RS", 0, 256), ("RS", 0, 256))
     op("g", g.iota, (T.QI[:, 0:2], [[0, 2]], 0, 1), [], [("QI", 0, 2)])
     op("g", g.iota, (T.ULI[:, 0:8], [[16, 8]], 0, 0), [], [("ULI", 0, 8)])
     op("g", g.affine_select, (T.DG[:, 0:528], T.ONE[:, 0:528], [[-1, 528]], AluOpType.is_equal, 0.0, 3, 4),
@@ -199,13 +201,14 @@ def rank_program(g, core, T, topo):
     vcopy(("QF", 0, 2), ("QJ", 0, 2))
     op("v", g.vector.tensor_scalar, (T.MK[:, 0:256], T.J16[:, 0:256], T.QF[:, 0:1], None, AluOpType.is_equal),
        [("J16", 0, 256), ("QF", 0, 2)], [MK])
-    ts(("RS", 0, 256), ("J16", 0, 256), 0.0, AluOpType.not_equal)
     vcopy(L("u", 0, 0, 8), ("ULI", 0, 8))
     for name, base in (("DA", 0), ("DB", 2)):
         for k, c in ((0, 0.0), (2, -1.0), (3, 1.0)):
             a = (base + k) % 4
             op("v", g.vector.memset, (T[name][:, a:512:4], c), [], [(name, a, 512, 4)])
     op("v", g.vector.memset, (T.TG[:, 256:512], 0.0), [], [("TG", 256, 512)])
+    for b in range(4):
+        quant(("QC", 128 * b, 128 * b + 128), ("SC", 128 * b, 128 * b + 128), ("DG", 3 - b, 515 - b))
 
     def couples(t):
         return (2, 127) if t % 2 else (0, 128)
@@ -224,11 +227,12 @@ def rank_program(g, core, T, topo):
         tt(("DD", 0, nc), ("ZP", k0, k0 + 2 * nc, 2), ("ZP", k0 + 1, min(k0 + 2 * nc + 1, 256), 2), SUB)
         op("s", g.scalar.activation, (T.AB[:, 0:nc], T.DD[:, 0:nc], ABS), [("DD", 0, nc)], [("AB", 0, nc)], bias=-128.0)
 
-    def kinds(t):
+    def kinds(t, w):
         nc = couples(t)[1]
-        ts(("NM", 0, nc), ("DD", 0, nc), 256.0, AluOpType.not_equal)
-        ts(("NE", 0, nc), ("AB", 0, nc), 127.5, AluOpType.is_lt)
-        ts(("WSG", 0, nc), ("AB", 0, nc), 128.5, AluOpType.is_gt)
+        if w == 0:
+            ts(("NE", 0, nc), ("AB", 0, nc), 127.5, AluOpType.is_lt)
+        else:
+            ts(("WSG", 0, nc), ("AB", 0, nc), 128.5, AluOpType.is_gt)
 
     def step_o(t):
         base, nc = couples(t)
@@ -243,33 +247,39 @@ def rank_program(g, core, T, topo):
     def weigh(t):
         base, nc = couples(t)
         end = base + 4 * nc
-        tt(("D1M", base, end, 4), ("WSG", 0, nc), ("DM", 0, nc), MUL)
         tt(("D1U", base, end, 4), ("NE", 0, nc), ("DO", 0, nc), MUL)
+        tt(("D1M", base, end, 4), ("WSG", 0, nc), ("DM", 0, nc), MUL)
+
+    def scores(t, q):
+        mm(7, 256, ("QR", 0, 128), ("SR", 0, 128), ("QX", 0, 256), ("SX", 0, 256))
+        from_bank(q, ("SS", 0, 256), 7, 256)
+        op("v", g.vector.tensor_copy, (T.SP[:, 0:128], T.SS[:, 0:256].indirect(vw(L("o", t, 0, 8)))),
+           [("SS", 0, 256), L("o", t, 0, 8)], [("SP", 0, 128)])
 
     vcopy(L("o", 0), ("OI", 0, 16))
     vcopy(L("m", 0), ("MI", 0, 16))
     op("v", g.vector.tensor_copy, (T.PR[:, 0:256].indirect(vw(L("o", 0))), T.IO[:, 0:256]), [IO, L("o", 0)], [PR])
     sgather(("PM", 0, 256), PR, L("m", 0))
-    quant(("QX", 0, 256), ("SX", 0, 256), ("XA", 0, 1024))
     quant(("QU", 0, 128), ("SU", 0, 128), ("UT", 0, 512))
-    tt(("SD", 0, 256), ("PM", 0, 256), PR, AluOpType.is_gt)
     ul = L("u", 0, 0, 8)
     op("s", g.scalar.activation, (T.SR[:, 0:128], T.SU[:, 0:128].indirect(vw(ul)), COPY),
        [("SU", 0, 128), ul], [("SR", 0, 128)])
+    op("v", g.vector.tensor_copy, (T.QR[:, 0:128].bitcast(dt.uint32), T.QU[:, 0:128].bitcast(dt.uint32).indirect(vw(ul))),
+       [("QU", 0, 128), ul], [("QR", 0, 128)])
+    quant(("QX", 0, 256), ("SX", 0, 256), ("XA", 0, 1024))
+    tt(("SD", 0, 256), ("PM", 0, 256), PR, AluOpType.is_gt)
     row("D1U", "US", IO, L("o", 0), 0)
     ts(("CL", 0, 128), ("SD", 0, 128), 1279.0, MUL)
     ts(("CL", 128, 256), ("SD", 128, 256), -769.0, MUL, 1024.0, ADD)
     ttg(("ZI", 0, 256), PR, L("m", 0), ("CL", 0, 256), ADD)
     sgather(("ZP", 0, 256), ("ZI", 0, 256), L("o", 0))
+    scores(0, "v")
     row("D1M", "MS", ("PM", 0, 256), L("o", 0), 0)
-    op("v", g.vector.tensor_copy, (T.QR[:, 0:128].bitcast(dt.uint32), T.QU[:, 0:128].bitcast(dt.uint32).indirect(vw(ul))),
-       [("QU", 0, 128), ul], [("QR", 0, 128)])
-    for b in range(4):
-        quant(("QC", 128 * b, 128 * b + 128), ("SC", 128 * b, 128 * b + 128), ("DG", 3 - b, 515 - b))
-    zdiff(0)
     step_o(0)
-    kinds(0)
+    zdiff(0)
     step_m(0)
+    kinds(0, 0)
+    kinds(0, 1)
     weigh(0)
 
     for t in range(3):
@@ -284,40 +294,35 @@ def rank_program(g, core, T, topo):
         def plane_h(b):
             return ("VW", 384 * b, 384 * b + 256)
 
-        def a_half(b):
-            sgather(("AH", 256 * b, 256 * b + 256), plane_h(b), L("m", t))
+        def a_half(b, x=0, y=256):
+            sgather(("AH", 256 * b + x, 256 * b + y), plane_h(b), L("m", t, x // 16, y // 16))
 
         def a_full(b):
             scopy(("AF", 256 * b, 256 * b + 256), ("AH", 256 * b, 256 * b + 256), 2.0)
 
-        mm(7, 256, ("QR", 0, 128), ("SR", 0, 128), ("QX", 0, 256), ("SX", 0, 256))
+        if t:
+            scores(t, "s")
         for b in range(4):
             mm(b, 256, ("QC", 128 * b, 128 * b + 128), ("SC", 128 * b, 128 * b + 128), ("QX", 0, 256), ("SX", 0, 256))
-        from_bank("s", ("SS", 0, 256), 7, 256)
-        op("v", g.vector.tensor_copy, (T.SP[:, 0:128], T.SS[:, 0:256].indirect(vw(L("o", t, 0, 8)))),
-           [("SS", 0, 256), L("o", t, 0, 8)], [("SP", 0, 128)])
         sgather(("SP", 128, 256), ("SS", 0, 256), L("o", t, 8, 16))
         for b in range(4):
             from_bank("s", plane_h(b), b, 256, 0.5)
-        a_half(0)
+        a_half(0, 0, 128)
         TR = (D0, base + 1, end, 4)
         tt(TR, ("SP", k0, e, 2), ("SP", k0 + 1, min(e + 1, 256), 2), AluOpType.is_gt)
         h = base + 4 * 64
         scan(("MS", base, h), (D0, base, h), ("D1M", base, h))
         scan(("US", base, end), (D0, base, end), ("D1U", base, end))
 
-        def mates_places(a, b):
-            tt(("MM", a, b), ("MS", 2 * a + 1, 2 * b, 2), ("MK", a, b), MUL)
-            segsum("MW", "MM", a, b)
-            ts(L("M", t, a // 16, b // 16), wrapped("MW", a, b), 2.0, MUL, 1.0, ADD)
-
-        def gives(a, b):
-            ttg(("GM", a, b), ("US", 0, 512), L("M", t, a // 16, b // 16), ("MK", a, b), MUL)
-            segsum("GW", "GM", a, b)
-            vcopy(L("g", t, a // 16, b // 16), wrapped("GW", a, b))
-
-        mates_places(0, 128)
-        gives(0, 128)
+        a, b = 0, 128
+        tt(("MM", a, b), ("MS", 2 * a + 1, 2 * b, 2), ("MK", a, b), MUL)
+        ts(("NM", 0, nc), ("DD", 0, nc), 256.0, AluOpType.not_equal)
+        segsum("MW", "MM", a, b)
+        scan(("MS", h, end), (D0, h, end), ("D1M", h, end))
+        ts(L("M", t, a // 16, b // 16), wrapped("MW", a, b), 2.0, MUL, 1.0, ADD)
+        ttg(("GM", a, b), ("US", 0, 512), L("M", t, a // 16, b // 16), ("MK", a, b), MUL)
+        segsum("GW", "GM", a, b)
+        vcopy(L("g", t, a // 16, b // 16), wrapped("GW", a, b))
         for b in range(2):
             op("v", g.vector.tensor_scalar, (T.ET[:, b:512:4], vw(plane_h(b)).indirect(vw(L("g", t, 0, 8))), 2.0, None, MUL),
                [plane_h(b), L("g", t, 0, 8)], [("ET", b, 512, 4)])
@@ -338,56 +343,60 @@ def rank_program(g, core, T, topo):
         tg = 256 * k0
         tt(("TG", tg + k0, tg + e, 2), TR, ("NM", 0, nc), MUL)
         scopy(("TG", tg + k0 + 1, tg + min(e + 1, 256), 2), ("TG", tg + k0, tg + e, 2), -1.0)
-        a_half(1)
-        scan(("MS", h, end), (D0, h, end), ("D1M", h, end))
+        if t == 0:
+            for a, b, k, c in ((0, 128, 769.0, 255.0), (128, 256, -1279.0, 1279.0)):
+                op("s", g.scalar.activation, (T.CM[:, a:b], T.SD[:, a:b], COPY), [("SD", a, b)], [("CM", a, b)], bias=c, scale=k)
+        a_half(0, 128, 256)
+        a, b = 128, 256
         if t == 0:
             tt(("NK", 0, 256), PR, MK, MUL)
-        mates_places(128, 256)
+        tt(("MM", a, b), ("MS", 2 * a + 1, 2 * b, 2), ("MK", a, b), MUL)
         if t == 0:
             segsum("NW", "NK", 0, 256)
+        segsum("MW", "MM", a, b)
+        if t == 0:
             vcopy(L("p", 0), wrapped("NW"))
             ts(("PF", 0, 16), wrapped("NW"), 256.0, ADD)
+        ts(L("M", t, a // 16, b // 16), wrapped("MW", a, b), 2.0, MUL, 1.0, ADD)
         sgather(("GU", 0, 256), ("US", 0, 512), L("M", t))
+        a_half(1)
         ttg(("PK", 0, 256), ("TG", tg, tg + 256), L("p", t), MK, MUL)
+        ttg(("GM", a, b), ("US", 0, 512), L("M", t, a // 16, b // 16), ("MK", a, b), MUL)
         segsum("PW", "PK", 0, 256)
-        if t == 0:
-            ts(("CM", 0, 128), ("SD", 0, 128), 769.0, MUL, 255.0, ADD)
-            ts(("CM", 128, 256), ("SD", 128, 256), -1279.0, MUL, 1279.0, ADD)
+        segsum("GW", "GM", a, b)
         pf, pf2 = ("PF", 16 * t, 16 * t + 16), ("PF", 16 * t + 16, 16 * t + 32)
         tt(pf2, pf, wrapped("PW"), ADD)
+        vcopy(L("g", t, a // 16, b // 16), wrapped("GW", a, b))
         ts(L("p", t + 1), pf2, -256.0, ADD)
         ts(("NB", 0, 16), pf2, 384.0, AluOpType.is_ge, -1000.0, MUL)
-        ttg(("NK", 0, 256), ("GU", 0, 256), L("p", t + 1), MK, MUL)
         if not last:
             sgather(PR, IO, L("p", t + 1))
-        segsum("NW", "NK", 0, 256)
+            ttg(("ZI", 0, 256), IO, L("p", t + 1), ("CM", 0, 256), ADD)
+            sgather(("ZP", 0, 256), ("ZI", 0, 256), L("g", t))
+        ttg(("NK", 0, 256), ("GU", 0, 256), L("p", t + 1), MK, MUL)
         tt(("NZ", 0, 16), ("NB", 0, 16), pf2, ADD)
+        segsum("NW", "NK", 0, 256)
         vcopy(L("m", t + 1), wrapped("NW"))
         sgather(("MR", 0, 256), IO, L("m", t + 1))
-        if not last:
-            ttg(("ZI", 0, 256), IO, L("p", t + 1), ("CM", 0, 256), ADD)
-        tt(("IX", 0, 16), ("NZ", 0, 16), wrapped("NW"), MAX)
-        gives(128, 256)
-        vcopy(L("i", t), ("IX", 0, 16))
-        if not last:
-            sgather(("ZP", 0, 256), ("ZI", 0, 256), L("g", t))
-        ttg(("OK", 0, 256), ("MR", 0, 256), L("g", t), MK, MUL)
         a_half(2)
-        segsum("OW", "OK", 0, 256)
+        tt(("IX", 0, 16), ("NZ", 0, 16), wrapped("NW"), MAX)
         if not last:
             zdiff(t + 1)
-        vcopy(L("o", t + 1), wrapped("OW"))
+        vcopy(L("i", t), ("IX", 0, 16))
+        a_half(3)
         if not last:
-            kinds(t + 1)
+            ttg(("OK", 0, 256), ("MR", 0, 256), L("g", t), MK, MUL)
+            segsum("OW", "OK", 0, 256)
         else:
             quant(("QV", 0, 128), ("SV", 0, 128), ("VT", 0, 512))
-        a_half(3)
         ED = [4, 5, 6, 0]
         for b in range(4):
             mm(ED[b], 128, ("QC", 128 * b, 128 * b + 128), ("SC", 128 * b, 128 * b + 128), ("EL%d" % t, 0, 128), ("ES%d" % t, 0, 128),
                [("arr%d" % t, lanes)])
         for b in range(4):
-            from_bank("vvss"[b], ("VW", 384 * b + 256, 384 * b + 384), ED[b], 128, 0.5)
+            if b == 3 and not last:
+                vcopy(L("o", t + 1), wrapped("OW"))
+            from_bank("vvvs"[b], ("VW", 384 * b + 256, 384 * b + 384), ED[b], 128, 0.5)
         if not last:
             row("D1U", "US", IO, L("o", t + 1), t + 1)
             row("D1M", "MS", PR, L("g", t), t + 1)
@@ -411,12 +420,19 @@ def rank_program(g, core, T, topo):
         if not last:
             step_o(t + 1)
             step_m(t + 1)
+        else:
+            ttg(("OK", 0, 256), ("MR", 0, 256), L("g", t), MK, MUL)
+            segsum("OW", "OK", 0, 256)
         for b in range(4):
             ttg(("XT", b, 1024, 4), ("GS", 256 * b, 256 * b + 256), L("m", t + 1), ("AF", 256 * b, 256 * b + 256), ADD)
+        if not last:
+            kinds(t + 1, 0)
         quant(("QX", 0, 256), ("SX", 0, 256), ("XT", 0, 1024))
         if not last:
+            kinds(t + 1, 1)
             weigh(t + 1)
         else:
+            vcopy(L("o", 3), wrapped("OW"))
             sgather(("OMR", 0, 256), IO, L("o", 3))
             sgather(("OMR", 256, 512), IO, L("m", 3))
             dma("y", T.om[:, 0:512], T.OMR[0:128:16, 0:512], [("OMR", 0, 512)], [])

from concourse.bass import DstId, RemoteDMATransfer
from concourse.mybir import dt, AluOpType, ActivationFunctionType

STEP = [1, 2, 4]
C = 256
X4 = "float8_e4m3fn_x4"

SCRATCH = {
    "XA": ("sbuf", [128, 1024], "bfloat16"), "XT": ("sbuf", [128, 1024], "bfloat16"),
    "UT": ("sbuf", [128, 512], "bfloat16"), "VT": ("sbuf", [128, 512], "bfloat16"),
    "ZT": ("sbuf", [128, 1024], "bfloat16"), "ET": ("sbuf", [128, 512], "bfloat16"),
    "ONE": ("sbuf", [128, 528], "bfloat16"), "DG": ("sbuf", [128, 528], "bfloat16"),
    "QX": ("sbuf", [128, 256], X4), "SX": ("sbuf", [128, 256], "uint8"),
    "QZ": ("sbuf", [128, 256], X4), "SZ": ("sbuf", [128, 256], "uint8"),
    "QU": ("sbuf", [128, 128], X4), "SU": ("sbuf", [128, 128], "uint8"),
    "QR": ("sbuf", [128, 128], X4), "SR": ("sbuf", [128, 128], "uint8"),
    "QV": ("sbuf", [128, 128], X4), "SV": ("sbuf", [128, 128], "uint8"),
    "QC": ("sbuf", [128, 512], X4), "SC": ("sbuf", [128, 512], "uint8"),
    "QW": ("sbuf", [128, 512], X4), "SW": ("sbuf", [128, 512], "uint8"),
    "VW": ("sbuf", [128, 4 * 384], "bfloat16"),
    "AH": ("sbuf", [128, 1024], "bfloat16"), "AF": ("sbuf", [128, 1024], "bfloat16"),
    "GS": ("sbuf", [128, 1024], "float32"), "YS": ("sbuf", [128, 256], "float32"),
    "OI": ("sbuf", [128, 16], "int32"), "MI": ("sbuf", [128, 16], "int32"),
    "LU": ("sbuf", [128, 24 * 16], "uint16"), "ULI": ("sbuf", [128, 8], "int32"),
    "QI": ("sbuf", [128, 2], "int32"), "QJ": ("sbuf", [128, 2], "int32"), "QF": ("sbuf", [128, 2], "float32"),
    "IO": ("sbuf", [128, 256], "bfloat16"), "J16": ("sbuf", [128, 256], "bfloat16"),
    "MK": ("sbuf", [128, 256], "bfloat16"), "RS": ("sbuf", [128, 256], "bfloat16"),
    "DA": ("sbuf", [128, 512], "bfloat16"), "DB": ("sbuf", [128, 512], "bfloat16"),
    "SS": ("sbuf", [128, 256], "float32"), "SP": ("sbuf", [128, 256], "float32"),
    "D1U": ("sbuf", [128, 512], "bfloat16"), "D1M": ("sbuf", [128, 512], "bfloat16"),
    "US": ("sbuf", [128, 512], "bfloat16"), "MS": ("sbuf", [128, 512], "bfloat16"),
    "MM": ("sbuf", [128, 256], "bfloat16"), "MW": ("sbuf", [128, 256], "bfloat16"),
    "GM": ("sbuf", [128, 256], "bfloat16"), "GW": ("sbuf", [128, 256], "bfloat16"),
    "TG": ("sbuf", [128, 512], "bfloat16"),
    "PK": ("sbuf", [128, 256], "bfloat16"), "PW": ("sbuf", [128, 256], "bfloat16"), "PF": ("sbuf", [128, 64], "float32"),
    "GU": ("sbuf", [128, 256], "bfloat16"), "NK": ("sbuf", [128, 256], "bfloat16"), "NW": ("sbuf", [128, 256], "bfloat16"),
    "NB": ("sbuf", [128, 16], "float32"), "NZ": ("sbuf", [128, 16], "float32"), "IX": ("sbuf", [128, 16], "float32"),
    "MR": ("sbuf", [128, 256], "bfloat16"), "OK": ("sbuf", [128, 256], "bfloat16"), "OW": ("sbuf", [128, 256], "bfloat16"),
    "PR": ("sbuf", [128, 256], "bfloat16"), "PM": ("sbuf", [128, 256], "bfloat16"), "SD": ("sbuf", [128, 256], "bfloat16"),
    "CL": ("sbuf", [128, 256], "float32"), "CM": ("sbuf", [128, 256], "float32"),
    "ZI": ("sbuf", [128, 256], "float32"), "ZP": ("sbuf", [128, 256], "float32"),
    "DD": ("sbuf", [128, 128], "float32"), "AB": ("sbuf", [128, 128], "float32"),
    "NE": ("sbuf", [128, 128], "bfloat16"), "NM": ("sbuf", [128, 128], "bfloat16"), "WSG": ("sbuf", [128, 128], "bfloat16"),
    "DO": ("sbuf", [128, 128], "bfloat16"), "DM": ("sbuf", [128, 128], "bfloat16"),
    "OMR": ("sbuf", [128, 512], "float32"),
}
for _t in range(3):
    SCRATCH["QE%d" % _t] = ("sbuf", [128, 128], X4)
    SCRATCH["SE%d" % _t] = ("sbuf", [128, 128], "uint8")
    SCRATCH["EL%d" % _t] = ("sbuf", [128, 128], X4)
    SCRATCH["ES%d" % _t] = ("sbuf", [128, 128], "uint8")
for _t in range(8):
    SCRATCH["B%d" % _t] = ("psum", [128, 512], "float32")
NDMA = 16
SEMAPHORES = ["cv", "cs", "ct", "cg", "loc"] + ["arr%d" % t for t in range(3)] + ["dm%d" % t for t in range(NDMA)]


def rank_program(g, core, T, topo):
    rank = T.rank_of(core)
    if rank is None:
        return
    ADD, SUB, MUL, MAX = AluOpType.add, AluOpType.subtract, AluOpType.mult, AluOpType.max
    COPY, ABS = ActivationFunctionType.Copy, ActivationFunctionType.Abs
    queue = {"v": g.vector, "s": g.scalar, "t": g.tensor, "g": g, "y": g.sync}
    total = {}
    seen = {q: {} for q in queue}
    acc = {}

    def meet(a, b):
        if a[0] >= b[1] or b[0] >= a[1]:
            return False
        return not (a[2] == b[2] and a[2] > 1 and (a[0] - b[0]) % a[2])

    def norm(r):
        return r[0], (r[1], r[2], r[3] if len(r) > 3 else 1)

    def wait(q, sem, val):
        if seen[q].get(sem, 0) < val:
            queue[q].wait_ge(T.sem[sem], val)
            seen[q][sem] = val

    def before(q, R, W, extra=()):
        dep = {}
        for regs, write in ((R, False), (W, True)):
            for r in regs:
                name, s = norm(r)
                excl = write or name[0] == "B" and name[1:].isdigit()
                for (s2, w2, sem, val) in acc.get(name, []):
                    if (excl or w2) and meet(s, s2):
                        dep[sem] = max(dep.get(sem, 0), val)
        for sem, val in extra:
            dep[sem] = max(dep.get(sem, 0), val)
        for sem in sorted(dep):
            wait(q, sem, dep[sem])

    def after(sem, val, R, W):
        for r in W:
            name, s = norm(r)
            acc[name] = [e for e in acc.get(name, []) if not (s[0] <= e[0][0] and e[0][1] <= s[1] and
                         (s[2] == 1 or s[2] == e[0][2] and (s[0] - e[0][0]) % s[2] == 0))]
        for regs, w in ((R, False), (W, True)):
            for r in regs:
                name, s = norm(r)
                acc.setdefault(name, []).append((s, w, sem, val))

    def op(q, call, args, R, W, extra=(), **kw):
        before(q, R, W, extra)
        sem = "c" + q
        call(*args, **kw).then_inc(T.sem[sem], 1)
        total[sem] = total.get(sem, 0) + 1
        after(sem, total[sem], R, W)

    ndma = [0]

    def dma(q, out, in_, R, W):
        before(q, R, W)
        sem = "dm%d" % ndma[0]
        ndma[0] += 1
        queue[q].dma_start(out, in_).then_inc(T.sem[sem], 16)
        total[sem] = 16
        after(sem, 16, R, W)

    def vw(r):
        name, (a, b, s) = norm(r)
        return T[name][:, a:b] if s == 1 else T[name][:, a:b:s]

    def tt(out, a, b, o):
        op("v", g.vector.tensor_tensor, (vw(out), vw(a), vw(b), o), [a, b], [out])

    def ttg(out, win, off, b, o):
        op("v", g.vector.tensor_tensor, (vw(out), vw(win).indirect(vw(off)), vw(b), o), [win, off, b], [out])

    def ts(out, a, s1, o1, s2=None, o2=None):
        if o2 is None:
            op("v", g.vector.tensor_scalar, (vw(out), vw(a), s1, None, o1), [a], [out])
        else:
            op("v", g.vector.tensor_scalar, (vw(out), vw(a), s1, s2, o1, o2), [a], [out])

    def vcopy(out, a):
        op("v", g.vector.tensor_copy, (vw(out), vw(a)), [a], [out])

    def scopy(out, a, scale=1.0):
        op("s", g.scalar.activation, (vw(out), vw(a), COPY), [a], [out], scale=scale)

    def sgather(out, win, off, scale=1.0):
        op("s", g.scalar.activation, (vw(out), vw(win).indirect(vw(off)), COPY), [win, off], [out], scale=scale)

    def scan(out, d0, d1):
        op("v", g.vector.tensor_tensor_scan, (vw(out), vw(d0), vw(d1), 0.0, MUL, ADD), [d0, d1], [out])

    def quant(codes, plane, tile):
        op("v", g.vector.quantize_mx, (vw(codes), vw(plane), vw(tile)), [tile], [codes, plane])

    def mm(bank, n, lc, ls, rc, rs, extra=()):
        b = ("B%d" % bank, 0, 512)
        op("t", g.tensor.matmul_mx, (T["B%d" % bank][:, 0:n], vw(lc), vw(ls), vw(rc), vw(rs), True, True),
           [lc, ls, rc, rs], [b], extra)

    def from_bank(q, out, bank, n, scale=1.0):
        b = ("B%d" % bank, 0, 512)
        src = T["B%d" % bank][:, 0:n]
        if q == "s":
            op("s", g.scalar.activation, (vw(out), src, COPY), [b], [out], scale=scale)
        elif scale == 1.0:
            op("v", g.vector.tensor_copy, (vw(out), src), [b], [out])
        else:
            op("v", g.vector.tensor_scalar, (vw(out), src, scale, None, MUL), [b], [out])

    place = {}

    def L(kind, t, a=0, b=16):
        k = place.setdefault((kind, t), len(place))
        return ("LU", 16 * k + a, 16 * k + b)

    IO, MK, PR = ("IO", 0, 256), ("MK", 0, 256), ("PR", 0, 256)

    def wrapped(name, a=0, b=256):
        return (name, a + 15, b, 16)

    def segsum(out, src, a, b):
        scan((out, a, b), ("RS", a, b), (src, a, b))

    dma("y", T.OI[:, 0:16], T.o[:, 0:16], [], [("OI", 0, 16)])
    dma("s", T.MI[:, 0:16], T.m[:, 0:16], [], [("MI", 0, 16)])
    dma("y", T.XA[:, 0:1024], T.x[:, 0:1024], [], [("XA", 0, 1024)])
    dma("s", T.UT[:, 0:512], T.u[:, 0:512], [], [("UT", 0, 512)])
    dma("y", T.QW[:, 0:512].bitcast(dt.uint8), T.wc[:, 0:2048], [], [("QW", 0, 512)])
    dma("y", T.SW[:, 0:512], T.ws[:, 0:512], [], [("SW", 0, 512)])
    dma("y", T.VT[:, 0:512], T.v[:, 0:512], [], [("VT", 0, 512)])

    op("v", g.vector.memset, (T.ONE[:, 0:528], 1.0), [], [("ONE", 0, 528)])
    op("v", g.vector.memset, (T.RS[:, 0:256], 1.0), [], [("RS", 0, 256)])
    op("v", g.vector.memset, (T.RS[:, 0:256:16], 0.0), [], [("RS", 0, 256, 16)])
    op("v", g.vector.tensor_tensor_scan, (T.IO[:, 0:256], T.ONE[:, 0:256], T.ONE[:, 0:256], -1.0, MUL, ADD), [("ONE", 0, 256)], [IO])
    scan(("J16", 0, 256), ("RS", 0, 256), ("RS", 0, 256))
    op("g", g.iota, (T.QI[:, 0:2], [[0, 2]], 0, 1), [], [("QI", 0, 2)])
    op("g", g.iota, (T.ULI[:, 0:8], [[16, 8]], 0, 0), [], [("ULI", 0, 8)])
    op("g", g.affine_select, (T.DG[:, 0:528], T.ONE[:, 0:528], [[-1, 528]], AluOpType.is_equal, 0.0, 3, 4),
       [("ONE", 0, 528)], [("DG", 0, 528)])
    ts(("QJ", 0, 2), ("QI", 0, 2), 15, AluOpType.bitwise_and)
    vcopy(("QF", 0, 2), ("QJ", 0, 2))
    op("v", g.vector.tensor_scalar, (T.MK[:, 0:256], T.J16[:, 0:256], T.QF[:, 0:1], None, AluOpType.is_equal),
       [("J16", 0, 256), ("QF", 0, 2)], [MK])
    vcopy(L("u", 0, 0, 8), ("ULI", 0, 8))
    for name, base in (("DA", 0), ("DB", 2)):
        for k, c in ((0, 0.0), (2, -1.0), (3, 1.0)):
            a = (base + k) % 4
            op("v", g.vector.memset, (T[name][:, a:512:4], c), [], [(name, a, 512, 4)])
    op("v", g.vector.memset, (T.TG[:, 256:512], 0.0), [], [("TG", 256, 512)])
    for b in range(4):
        quant(("QC", 128 * b, 128 * b + 128), ("SC", 128 * b, 128 * b + 128), ("DG", 3 - b, 515 - b))

    def couples(t):
        return (2, 127) if t % 2 else (0, 128)

    def row(name, keep, win, off, t):
        base, nc = couples(t)
        end = base + 4 * nc
        sgather((name, 1, 512, 2), win, off)
        scopy((name, base + 2, end, 4), (name, base + 1, end, 4))
        if t % 2:
            scopy((keep, 1, 512, 510), (name, 1, 512, 510))

    def zdiff(t):
        k0 = t % 2
        nc = couples(t)[1]
        tt(("DD", 0, nc), ("ZP", k0, k0 + 2 * nc, 2), ("ZP", k0 + 1, min(k0 + 2 * nc + 1, 256), 2), SUB)
        op("s", g.scalar.activation, (T.AB[:, 0:nc], T.DD[:, 0:nc], ABS), [("DD", 0, nc)], [("AB", 0, nc)], bias=-128.0)

    def kinds(t, w):
        nc = couples(t)[1]
        if w == 0:
            ts(("NE", 0, nc), ("AB", 0, nc), 127.5, AluOpType.is_lt)
        else:
            ts(("WSG", 0, nc), ("AB", 0, nc), 128.5, AluOpType.is_gt)

    def step_o(t):
        base, nc = couples(t)
        end = base + 4 * nc
        tt(("DO", 0, nc), ("D1U", base + 3, end, 4), ("D1U", base + 1, end, 4), SUB)

    def step_m(t):
        base, nc = couples(t)
        end = base + 4 * nc
        tt(("DM", 0, nc), ("D1M", base + 3, end, 4), ("D1M", base + 1, end, 4), SUB)

    def weigh(t):
        base, nc = couples(t)
        end = base + 4 * nc
        tt(("D1U", base, end, 4), ("NE", 0, nc), ("DO", 0, nc), MUL)
        tt(("D1M", base, end, 4), ("WSG", 0, nc), ("DM", 0, nc), MUL)

    def scores(t, q):
        mm(7, 256, ("QR", 0, 128), ("SR", 0, 128), ("QX", 0, 256), ("SX", 0, 256))
        from_bank(q, ("SS", 0, 256), 7, 256)
        op("v", g.vector.tensor_copy, (T.SP[:, 0:128], T.SS[:, 0:256].indirect(vw(L("o", t, 0, 8)))),
           [("SS", 0, 256), L("o", t, 0, 8)], [("SP", 0, 128)])

    vcopy(L("o", 0), ("OI", 0, 16))
    vcopy(L("m", 0), ("MI", 0, 16))
    op("v", g.vector.tensor_copy, (T.PR[:, 0:256].indirect(vw(L("o", 0))), T.IO[:, 0:256]), [IO, L("o", 0)], [PR])
    sgather(("PM", 0, 256), PR, L("m", 0))
    quant(("QU", 0, 128), ("SU", 0, 128), ("UT", 0, 512))
    ul = L("u", 0, 0, 8)
    op("s", g.scalar.activation, (T.SR[:, 0:128], T.SU[:, 0:128].indirect(vw(ul)), COPY),
       [("SU", 0, 128), ul], [("SR", 0, 128)])
    op("v", g.vector.tensor_copy, (T.QR[:, 0:128].bitcast(dt.uint32), T.QU[:, 0:128].bitcast(dt.uint32).indirect(vw(ul))),
       [("QU", 0, 128), ul], [("QR", 0, 128)])
    quant(("QX", 0, 256), ("SX", 0, 256), ("XA", 0, 1024))
    tt(("SD", 0, 256), ("PM", 0, 256), PR, AluOpType.is_gt)
    row("D1U", "US", IO, L("o", 0), 0)
    ts(("CL", 0, 128), ("SD", 0, 128), 1279.0, MUL)
    ts(("CL", 128, 256), ("SD", 128, 256), -769.0, MUL, 1024.0, ADD)
    ttg(("ZI", 0, 256), PR, L("m", 0), ("CL", 0, 256), ADD)
    sgather(("ZP", 0, 256), ("ZI", 0, 256), L("o", 0))
    scores(0, "v")
    row("D1M", "MS", ("PM", 0, 256), L("o", 0), 0)
    step_o(0)
    zdiff(0)
    step_m(0)
    kinds(0, 0)
    kinds(0, 1)
    weigh(0)

    for t in range(3):
        k0 = t % 2
        base, nc = couples(t)
        end = base + 4 * nc
        e = k0 + 2 * nc
        last = t == 2
        D0 = "DB" if t % 2 else "DA"
        partner = T.cores[rank ^ STEP[t]]

        def plane_h(b):
            return ("VW", 384 * b, 384 * b + 256)

        def a_half(b, x=0, y=256):
            sgather(("AH", 256 * b + x, 256 * b + y), plane_h(b), L("m", t, x // 16, y // 16))

        def a_full(b):
            scopy(("AF", 256 * b, 256 * b + 256), ("AH", 256 * b, 256 * b + 256), 2.0)

        if t:
            scores(t, "s")
        for b in range(4):
            mm(b, 256, ("QC", 128 * b, 128 * b + 128), ("SC", 128 * b, 128 * b + 128), ("QX", 0, 256), ("SX", 0, 256))
        sgather(("SP", 128, 256), ("SS", 0, 256), L("o", t, 8, 16))
        for b in range(4):
            from_bank("s", plane_h(b), b, 256, 0.5)
        a_half(0, 0, 128)
        TR = (D0, base + 1, end, 4)
        tt(TR, ("SP", k0, e, 2), ("SP", k0 + 1, min(e + 1, 256), 2), AluOpType.is_gt)
        h = base + 4 * 64
        scan(("MS", base, h), (D0, base, h), ("D1M", base, h))
        scan(("US", base, end), (D0, base, end), ("D1U", base, end))

        a, b = 0, 128
        tt(("MM", a, b), ("MS", 2 * a + 1, 2 * b, 2), ("MK", a, b), MUL)
        ts(("NM", 0, nc), ("DD", 0, nc), 256.0, AluOpType.not_equal)
        segsum("MW", "MM", a, b)
        scan(("MS", h, end), (D0, h, end), ("D1M", h, end))
        ts(L("M", t, a // 16, b // 16), wrapped("MW", a, b), 2.0, MUL, 1.0, ADD)
        ttg(("GM", a, b), ("US", 0, 512), L("M", t, a // 16, b // 16), ("MK", a, b), MUL)
        segsum("GW", "GM", a, b)
        vcopy(L("g", t, a // 16, b // 16), wrapped("GW", a, b))
        for b in range(2):
            op("v", g.vector.tensor_scalar, (T.ET[:, b:512:4], vw(plane_h(b)).indirect(vw(L("g", t, 0, 8))), 2.0, None, MUL),
               [plane_h(b), L("g", t, 0, 8)], [("ET", b, 512, 4)])
        for b in range(2, 4):
            sgather(("ET", b, 512, 4), plane_h(b), L("g", t, 0, 8), 2.0)
        QE, SE = ("QE%d" % t, 0, 128), ("SE%d" % t, 0, 128)
        quant(QE, SE, ("ET", 0, 512))
        before("g", [QE, SE], [])
        rid, pid = topo.addr(partner, core)
        mask = topo.mask(core, partner)
        g.remote_dma(T["EL%d" % t][:, 0:128].bitcast(dt.uint8), T["QE%d" % t][:, 0:128].bitcast(dt.uint8),
                     T.sem["arr%d" % t], T.sem["loc"], pid, rid, mask)
        g.remote_dma(T["ES%d" % t][:, 0:128], T["SE%d" % t][:, 0:128],
                     T.sem["arr%d" % t], T.sem["loc"], pid, rid, mask)
        lanes = 2 * len(topo.engines(core, partner))
        total["loc"] = total.get("loc", 0) + lanes

        tg = 256 * k0
        tt(("TG", tg + k0, tg + e, 2), TR, ("NM", 0, nc), MUL)
        scopy(("TG", tg + k0 + 1, tg + min(e + 1, 256), 2), ("TG", tg + k0, tg + e, 2), -1.0)
        if t == 0:
            for a, b, k, c in ((0, 128, 769.0, 255.0), (128, 256, -1279.0, 1279.0)):
                op("s", g.scalar.activation, (T.CM[:, a:b], T.SD[:, a:b], COPY), [("SD", a, b)], [("CM", a, b)], bias=c, scale=k)
        a_half(0, 128, 256)
        a, b = 128, 256
        if t == 0:
            tt(("NK", 0, 256), PR, MK, MUL)
        tt(("MM", a, b), ("MS", 2 * a + 1, 2 * b, 2), ("MK", a, b), MUL)
        if t == 0:
            segsum("NW", "NK", 0, 256)
        segsum("MW", "MM", a, b)
        if t == 0:
            vcopy(L("p", 0), wrapped("NW"))
            ts(("PF", 0, 16), wrapped("NW"), 256.0, ADD)
        ts(L("M", t, a // 16, b // 16), wrapped("MW", a, b), 2.0, MUL, 1.0, ADD)
        sgather(("GU", 0, 256), ("US", 0, 512), L("M", t))
        a_half(1)
        ttg(("PK", 0, 256), ("TG", tg, tg + 256), L("p", t), MK, MUL)
        ttg(("GM", a, b), ("US", 0, 512), L("M", t, a // 16, b // 16), ("MK", a, b), MUL)
        segsum("PW", "PK", 0, 256)
        segsum("GW", "GM", a, b)
        pf, pf2 = ("PF", 16 * t, 16 * t + 16), ("PF", 16 * t + 16, 16 * t + 32)
        tt(pf2, pf, wrapped("PW"), ADD)
        vcopy(L("g", t, a // 16, b // 16), wrapped("GW", a, b))
        ts(L("p", t + 1), pf2, -256.0, ADD)
        ts(("NB", 0, 16), pf2, 384.0, AluOpType.is_ge, -1000.0, MUL)
        if not last:
            sgather(PR, IO, L("p", t + 1))
            ttg(("ZI", 0, 256), IO, L("p", t + 1), ("CM", 0, 256), ADD)
            sgather(("ZP", 0, 256), ("ZI", 0, 256), L("g", t))
        ttg(("NK", 0, 256), ("GU", 0, 256), L("p", t + 1), MK, MUL)
        tt(("NZ", 0, 16), ("NB", 0, 16), pf2, ADD)
        segsum("NW", "NK", 0, 256)
        vcopy(L("m", t + 1), wrapped("NW"))
        sgather(("MR", 0, 256), IO, L("m", t + 1))
        a_half(2)
        tt(("IX", 0, 16), ("NZ", 0, 16), wrapped("NW"), MAX)
        if not last:
            zdiff(t + 1)
        vcopy(L("i", t), ("IX", 0, 16))
        a_half(3)
        if not last:
            ttg(("OK", 0, 256), ("MR", 0, 256), L("g", t), MK, MUL)
            segsum("OW", "OK", 0, 256)
        else:
            quant(("QV", 0, 128), ("SV", 0, 128), ("VT", 0, 512))
        ED = [4, 5, 6, 0]
        for b in range(4):
            mm(ED[b], 128, ("QC", 128 * b, 128 * b + 128), ("SC", 128 * b, 128 * b + 128), ("EL%d" % t, 0, 128), ("ES%d" % t, 0, 128),
               [("arr%d" % t, lanes)])
        for b in range(4):
            if b == 3 and not last:
                vcopy(L("o", t + 1), wrapped("OW"))
            from_bank("vvvs"[b], ("VW", 384 * b + 256, 384 * b + 384), ED[b], 128, 0.5)
        if not last:
            row("D1U", "US", IO, L("o", t + 1), t + 1)
            row("D1M", "MS", PR, L("g", t), t + 1)
        GB = [[1, 2, 3, 4], [5, 6, 0, 1]]
        for hh in range(2):
            for b in range(4):
                c0 = 256 * b + 128 * hh
                ttg(("ZT", 512 * hh + b, 512 * hh + 512, 4), ("VW", 384 * b, 384 * b + 384), L("i", t, 8 * hh, 8 * hh + 8),
                    ("AH", c0, c0 + 128), ADD)
            z = (128 * hh, 128 * hh + 128)
            quant(("QZ",) + z, ("SZ",) + z, ("ZT", 512 * hh, 512 * hh + 512))
            for b in range(4):
                mm(GB[hh][b], 128, ("QW", 128 * b, 128 * b + 128), ("SW", 128 * b, 128 * b + 128), ("QZ",) + z, ("SZ",) + z)
            for b in range(4):
                from_bank("s", ("GS", 256 * b + 128 * hh, 256 * b + 128 * hh + 128), GB[hh][b], 128, 0.0078125)
                if hh == 1 and b < 2:
                    a_full(b + 2)
            if hh == 0:
                a_full(0)
                a_full(1)
        if not last:
            step_o(t + 1)
            step_m(t + 1)
        else:
            ttg(("OK", 0, 256), ("MR", 0, 256), L("g", t), MK, MUL)
            segsum("OW", "OK", 0, 256)
        for b in range(4):
            ttg(("XT", b, 1024, 4), ("GS", 256 * b, 256 * b + 256), L("m", t + 1), ("AF", 256 * b, 256 * b + 256), ADD)
        if not last:
            kinds(t + 1, 0)
        quant(("QX", 0, 256), ("SX", 0, 256), ("XT", 0, 1024))
        if not last:
            kinds(t + 1, 1)
            weigh(t + 1)
        else:
            vcopy(L("o", 3), wrapped("OW"))
            sgather(("OMR", 0, 256), IO, L("o", 3))
            sgather(("OMR", 256, 512), IO, L("m", 3))
            dma("y", T.om[:, 0:512], T.OMR[0:128:16, 0:512], [("OMR", 0, 512)], [])

    mm(7, 256, ("QV", 0, 128), ("SV", 0, 128), ("QX", 0, 256), ("SX", 0, 256))
    from_bank("v", ("YS", 0, 256), 7, 256)
    dma("y", T.oc[:, 0:1024], T.QX[:, 0:256].bitcast(dt.uint8), [("QX", 0, 256)], [])
    for k in range(4):
        dma("s" if k % 2 else "y", T.osc[4 * k:4 * k + 4, 0:256], T.SX[32 * k:32 * k + 4, 0:256], [("SX", 0, 256)], [])
    dma("y", T.y[:, 0:256], T.YS[:, 0:256], [("YS", 0, 256)], [])
    for sem in sorted(total):
        wait("g", sem, total[sem])
